import numpy as np
import ml_dtypes


def mxq(x, axis, fmt="e4m3"):
    dtype, down = {"e4m3": (ml_dtypes.float8_e4m3fn, 7), "e5m2": (ml_dtypes.float8_e5m2, 14)}[fmt]
    v = np.moveaxis(np.asarray(x, np.float32).astype(ml_dtypes.bfloat16).astype(np.float64), axis, -1)
    blocks = v.reshape(v.shape[:-1] + (-1, 32))
    amax = np.abs(blocks).max(-1, keepdims=True)
    byte = np.maximum(np.where(amax > 0, np.frexp(amax)[1] - 1 + 127, 0) - down, 1)
    scale = np.exp2(byte - 127.0)
    codes = (blocks / scale).astype(np.float32).astype(dtype).astype(np.float64)
    return np.moveaxis((codes * scale).reshape(v.shape), -1, axis)


WIDE = False


def mx_kscale(k):
    if not WIDE:
        return np.ones(k)
    levels = np.array([10, -10, 5, -5, 0])
    if k % 512:
        return np.exp2(np.random.permutation(np.resize(levels, k // 32))).repeat(32)
    a = np.empty((k // 512, 16))
    for p in range(k // 512):
        a[p, :8] = np.random.permutation(np.resize(levels, 8))
        for g in range(8):
            far = levels[np.abs(levels - a[p, g]) >= 10]
            a[p, g + 8] = far[np.random.randint(len(far))]
    return np.exp2(a.ravel()).repeat(32)


def f64(x):
    return np.asarray(x).astype(np.float64)


def striped(idx):
    return np.tile(idx.reshape(-1, 16).T, (8, 1)).astype(np.uint16)


def unstriped(offs):
    return offs[:16].T.reshape(-1).astype(np.int64)


def pack_weight(w):
    k, n = w.shape
    w = f64(np.asarray(w, np.float32).astype(ml_dtypes.bfloat16)).reshape(k // 32, 32, n)
    amax = np.abs(w).max(1)
    byte = np.clip(np.where(amax > 0, np.frexp(amax)[1] - 1 + 127 - 7, 1), 1, 254)
    scaled = (w * np.exp2(127.0 - byte)[:, None, :]).reshape(k, n).astype(np.float32)
    words = np.ascontiguousarray(scaled.reshape(k // 512, 128, 4, n).transpose(0, 1, 3, 2)).astype(ml_dtypes.float8_e4m3fn).view(np.uint8)
    return words, np.ascontiguousarray(byte.astype(np.uint8).reshape(k // 512, 16, n))


def unpack_weight(words, scales):
    g, p, n, _ = words.shape
    vals = np.ascontiguousarray(words).view(ml_dtypes.float8_e4m3fn).astype(np.float64) * np.repeat(np.exp2(scales.astype(np.float64) - 127.0), 8, axis=1)[..., None]
    return vals.transpose(0, 1, 3, 2).reshape(g * 512, n)


K, T, E, C, N = 1536, 1024, 16, 128, 128


def by_expert(wq, xq):
    return np.concatenate([wq[e].T @ xq[:, e * C:(e + 1) * C] for e in range(E)], axis=1)


def setup_inputs():
    n = np.random.standard_normal
    s = mx_kscale(K)[:, None]
    first = np.random.permutation(np.repeat(np.arange(E), T // E))
    second = (first + 1 + np.random.permutation(np.repeat(np.arange(E - 1), -(-T // (E - 1)))[:T])) % E
    while np.bincount(second, minlength=E).max() != T // E:
        load = np.bincount(second, minlength=E); hi, lo = int(load.argmax()), int(load.argmin())
        t = np.flatnonzero((second == hi) & (first != lo))[0]; second[t] = lo
    slot_token = np.empty(E * C, np.int64); pos = np.empty((2, T), np.int64); fill = np.zeros(E, np.int64)
    place = np.stack([np.random.permutation(C) for _ in range(E)])
    for r, deal in enumerate((first, second)):
        for t in np.random.permutation(T):
            e = deal[t]; j = e * C + place[e, fill[e]]; fill[e] += 1; slot_token[j] = t; pos[r, t] = j
    g = np.random.uniform(0.2, 0.8, T)
    packed = [pack_weight(m) for m in n((E, K, N)) / np.sqrt(K) / s[None]]
    w_slot = np.empty(E * C); w_slot[pos[0]] = g; w_slot[pos[1]] = 1.0 - g
    return {
        "xT": (n((K, T)) * s).astype(np.float32),
        "w_words": np.stack([m[0] for m in packed]),
        "w_scales": np.stack([m[1] for m in packed]),
        "gate": np.tile(w_slot, (K, 1)).astype(np.float32),
        "offs": striped(slot_token),
        "pos1": striped(pos[0]),
        "pos2": striped(pos[1]),
    }


def reference(xT, w_words, w_scales, gate, offs, pos1, pos2):
    idx = unstriped(offs)
    w = np.stack([unpack_weight(w_words[e], w_scales[e]) for e in range(E)])
    xq = mxq(f64(gate) * f64(xT)[:, idx], 0, "e4m3")
    y = by_expert(w, xq)
    return y[:, unstriped(pos1)] + y[:, unstriped(pos2)]

@@ -1,0 +1,177 @@
+from contextlib import ExitStack
+
+import concourse.mybir as mybir
+
+K, T, E, C, N = 1536, 1024, 16, 128, 128
+S = E * C
+
+FLOPS = 2 * K * S * N
+BYTES = 4 * K * T + E * K * N + E * (K // 32) * N + 4 * S + 2 * 128 * (S + 2 * T) // 16 + 4 * N * T
+
+F32 = mybir.dt.float32
+BF16 = mybir.dt.bfloat16
+I32 = mybir.dt.int32
+U32 = mybir.dt.uint32
+U16 = mybir.dt.uint16
+U8 = mybir.dt.uint8
+FP8X4 = mybir.dt.float8_e4m3fn_x4
+MULT = mybir.AluOpType.mult
+ADD = mybir.AluOpType.add
+
+P = 128
+PACK = 4
+PASSES = K // (P * PACK)
+GROUP = 16
+PAD = 16
+HALF = S // 2
+HEAD = 256
+TAIL = 256
+BANK = 512
+
+STEPS = [(0, 0, 1024), (1, 0, 1024), (2, 0, 1024), (0, 1024, 1024), (1, 1024, 1024),
+         (2, 1024, 512), (2, 1536, 256), (2, 1792, 128), (2, 1920, 128)]
+
+
+def tile_moe_pre_lin_none_kernel(tc, xT, w_words, w_scales, gate, offs, pos1, pos2, out):
+    nc = tc.nc
+    with ExitStack() as ctx:
+        keep = ctx.enter_context(tc.tile_pool(name="keep", bufs=1))
+        stage = ctx.enter_context(tc.tile_pool(name="stage", bufs=3))
+        psum = ctx.enter_context(tc.psum_pool(name="psum", bufs=1))
+
+        slot_tokens = keep.tile([P, S // GROUP], U16, name="slot_tokens")
+        first_slots = keep.tile([P, T // GROUP], U16, name="first_slots")
+        second_slots = keep.tile([P, T // GROUP], U16, name="second_slots")
+        x_rows = [[keep.tile([P, T + PAD], F32, name="x_rows_%d_%d" % (a, r)) for r in range(PACK)] for a in range(PASSES)]
+        gates = keep.tile([P, S], F32, name="gates")
+        w_codes = keep.tile([P, E * PASSES, N], U32, name="w_codes", align_bytes=64)
+        w_plane = keep.tile([P, E * PASSES, N], U8, name="w_plane", align_bytes=64)
+        x_codes = keep.tile([P, PASSES, S], U32, name="x_codes", align_bytes=64)
+        x_plane = keep.tile([P, PASSES, S], U8, name="x_plane", align_bytes=64)
+        y = keep.tile([P, S], F32, name="y")
+
+        for a in range(PASSES):
+            for r in range(PACK):
+                nc.vector.memset(x_rows[a][r][:, T:], 0.0)
+        nc.vector.memset(w_plane[:].bitcast(I32), 0)
+
+        x_view = xT.rearrange("(a p r) t -> a r p t", p=P, r=PACK)
+        nc.sync.dma_start(out=x_rows[0][0][:, :T], in_=x_view[0, 0])
+        nc.sync.dma_start(slot_tokens[:], offs)
+        nc.sync.dma_start(out=gates[:, :HEAD], in_=gate[:P, :HEAD])
+        nc.sync.dma_start(out=gates[:, HEAD:HALF], in_=gate[:P, HEAD:HALF])
+        for a in range(PASSES):
+            for r in range(PACK):
+                if (a, r) != (0, 0):
+                    nc.sync.dma_start(out=x_rows[a][r][:, :T], in_=x_view[a, r])
+        nc.sync.dma_start(out=gates[:, HALF:], in_=gate[:P, HALF:])
+        scale_rows = w_scales.rearrange("e a q n -> q (e a) n")
+        for quad in range(4):
+            nc.sync.dma_start(out=w_plane[32 * quad : 32 * quad + 4].bitcast(I32),
+                              in_=scale_rows[4 * quad : 4 * quad + 4].bitcast(I32))
+        word_rows = w_words.rearrange("e a p n r -> p (e a) (n r)").bitcast(I32)
+        for j0 in range(0, E * PASSES, 4 * PASSES):
+            nc.sync.dma_start(out=w_codes[:, j0 : j0 + 4 * PASSES, :].bitcast(I32), in_=word_rows[:, j0 : j0 + 4 * PASSES, :])
+        nc.sync.dma_start(first_slots[:], pos1)
+        nc.sync.dma_start(second_slots[:], pos2)
+
+        rounded = {}
+        sums = {}
+
+        def gather(i):
+            a, s0, n = STEPS[i]
+            gated = stage.tile([P, PACK, n], F32, name="gated", tag="gated")
+            for r in range(PACK):
+                cuts = [0, HEAD, n] if (i, r) == (0, 0) else [0, n]
+                for c0, c1 in zip(cuts, cuts[1:]):
+                    nc.vector.tensor_tensor(
+                        gated[:, r, c0:c1],
+                        x_rows[a][r][:].indirect(slot_tokens[:, (s0 + c0) // GROUP : (s0 + c1) // GROUP]),
+                        gates[:, s0 + c0 : s0 + c1],
+                        MULT,
+                    )
+            rounded[i] = stage.tile([P, n, PACK], BF16, name="rounded", tag="rounded", align_bytes=64)
+            nc.scalar.copy(
+                out=rounded[i][:].rearrange("p (c i) r -> p c r i", i=4),
+                in_=gated[:].rearrange("p r (c i) -> p c r i", i=4),
+            )
+
+        def quantize(i):
+            a, s0, n = STEPS[i]
+            nc.vector.quantize_mx(
+                out=x_codes[:, a, s0 : s0 + n].bitcast(FP8X4),
+                scales=x_plane[:, a, s0 : s0 + n],
+                in_=rounded[i][:].rearrange("p n r -> p (n r)"),
+            )
+
+        def multiply(s0, n, passes):
+            if s0 not in sums:
+                sums[s0] = psum.tile([P, n], F32, name="sums_%d" % s0)
+            for e in range(s0 // C, (s0 + n) // C):
+                cols = slice(e * C, (e + 1) * C)
+                for a in passes:
+                    nc.tensor.matmul_mx(
+                        out=sums[s0][:, e * C - s0 : (e + 1) * C - s0],
+                        lhsT=w_codes[:, e * PASSES + a, :].bitcast(FP8X4),
+                        lhsT_scale=w_plane[:, e * PASSES + a, :],
+                        rhs=x_codes[:, a, cols].bitcast(FP8X4),
+                        rhs_scale=x_plane[:, a, cols],
+                        start=(a == 0),
+                        stop=(a == PASSES - 1),
+                    )
+
+        def copy_out(s0, n):
+            nc.scalar.copy(out=y[:, s0 : s0 + n], in_=sums[s0][:])
+
+        every = range(PASSES)
+        gather(0)
+        gather(1)
+        quantize(0)
+        gather(2)
+        quantize(1)
+        gather(3)
+        quantize(2)
+        multiply(0, BANK, every)
+        multiply(BANK, BANK, every)
+        gather(4)
+        copy_out(0, BANK)
+        copy_out(BANK, BANK)
+        quantize(3)
+        gather(5)
+        quantize(4)
+        multiply(1792, 128, [0, 1])
+        multiply(1920, 128, [0, 1])
+        gather(6)
+        quantize(5)
+        multiply(1024, 512, every)
+        gather(7)
+        copy_out(1024, 512)
+        gather(8)
+        quantize(6)
+        multiply(1536, 256, every)
+        quantize(7)
+        multiply(1792, 128, [2])
+        quantize(8)
+        multiply(1920, 128, [2])
+        copy_out(1536, 256)
+        copy_out(1792, 128)
+        copy_out(1920, 128)
+
+        y1 = keep.tile([P, T], F32, name="y1")
+        y2 = keep.tile([P, T], F32, name="y2")
+        total = keep.tile([P, T], F32, name="total")
+
+        def fetch(dst, slots, t0, t1):
+            nc.vector.tensor_copy(dst[:, t0:t1], y[:].indirect(slots[:, t0 // GROUP : t1 // GROUP]))
+
+        def combine(t0, t1):
+            nc.vector.tensor_tensor(total[:, t0:t1], y1[:, t0:t1], y2[:, t0:t1], ADD)
+            nc.sync.dma_start(out=out[:, t0:t1], in_=total[:, t0:t1])
+
+        cut = T - TAIL
+        fetch(y1, first_slots, 0, cut)
+        fetch(y2, second_slots, 0, cut)
+        fetch(y1, first_slots, cut, T)
+        combine(0, cut)
+        fetch(y2, second_slots, cut, T)
+        combine(cut, T)

@@ -24,12 +24,12 @@ PASSES = K // (P * PACK)
 GROUP = 16
 PAD = 16
 HALF = S // 2
-HEAD = 256
+HEAD = 320
 TAIL = 256
 BANK = 512
 
 STEPS = [(0, 0, 1024), (1, 0, 1024), (2, 0, 1024), (0, 1024, 1024), (1, 1024, 1024),
-         (2, 1024, 512), (2, 1536, 256), (2, 1792, 128), (2, 1920, 128)]
+         (2, 1024, 640), (2, 1664, 256), (2, 1920, 128)]
 
 
 def tile_moe_pre_lin_none_kernel(tc, xT, w_words, w_scales, gate, offs, pos1, pos2, out):
@@ -90,18 +90,20 @@ def tile_moe_pre_lin_none_kernel(tc, xT, w_words, w_scales, gate, offs, pos1, po
                         gates[:, s0 + c0 : s0 + c1],
                         MULT,
                     )
-            rounded[i] = stage.tile([P, n, PACK], BF16, name="rounded", tag="rounded", align_bytes=64)
+            h0 = s0 - s0 % HALF
+            if (a, h0) not in rounded:
+                rounded[(a, h0)] = stage.tile([P, HALF, PACK], BF16, name="rounded", tag="rounded", align_bytes=64)
             nc.scalar.copy(
-                out=rounded[i][:].rearrange("p (c i) r -> p c r i", i=4),
+                out=rounded[(a, h0)][:, s0 - h0 : s0 - h0 + n, :].rearrange("p (c i) r -> p c r i", i=4),
                 in_=gated[:].rearrange("p r (c i) -> p c r i", i=4),
             )
 
-        def quantize(i):
-            a, s0, n = STEPS[i]
+        def quantize(a, s0, n):
+            h0 = s0 - s0 % HALF
             nc.vector.quantize_mx(
                 out=x_codes[:, a, s0 : s0 + n].bitcast(FP8X4),
                 scales=x_plane[:, a, s0 : s0 + n],
-                in_=rounded[i][:].rearrange("p n r -> p (n r)"),
+                in_=rounded[(a, h0)][:, s0 - h0 : s0 - h0 + n, :].rearrange("p n r -> p (n r)"),
             )
 
         def multiply(s0, n, passes):
@@ -124,38 +126,38 @@ def tile_moe_pre_lin_none_kernel(tc, xT, w_words, w_scales, gate, offs, pos1, po
             nc.scalar.copy(out=y[:, s0 : s0 + n], in_=sums[s0][:])
 
         every = range(PASSES)
+        late = range(HALF + BANK, S, C)
         gather(0)
         gather(1)
-        quantize(0)
+        quantize(0, 0, HALF)
         gather(2)
-        quantize(1)
+        quantize(1, 0, HALF)
         gather(3)
-        quantize(2)
+        quantize(2, 0, HALF)
         multiply(0, BANK, every)
         multiply(BANK, BANK, every)
         gather(4)
         copy_out(0, BANK)
         copy_out(BANK, BANK)
-        quantize(3)
+        quantize(0, HALF, HALF)
         gather(5)
-        quantize(4)
-        multiply(1792, 128, [0, 1])
-        multiply(1920, 128, [0, 1])
+        quantize(1, HALF, HALF)
+        for s0 in late:
+            multiply(s0, C, [0, 1])
         gather(6)
-        quantize(5)
-        multiply(1024, 512, every)
+        quantize(2, HALF, BANK)
+        multiply(HALF, BANK, every)
         gather(7)
-        copy_out(1024, 512)
-        gather(8)
-        quantize(6)
-        multiply(1536, 256, every)
-        quantize(7)
-        multiply(1792, 128, [2])
-        quantize(8)
-        multiply(1920, 128, [2])
-        copy_out(1536, 256)
-        copy_out(1792, 128)
-        copy_out(1920, 128)
+        copy_out(HALF, BANK)
+        quantize(2, 1536, 256)
+        multiply(1536, C, [2])
+        multiply(1664, C, [2])
+        quantize(2, 1792, 128)
+        multiply(1792, C, [2])
+        quantize(2, 1920, 128)
+        multiply(1920, C, [2])
+        for s0 in late:
+            copy_out(s0, C)
 
         y1 = keep.tile([P, T], F32, name="y1")
         y2 = keep.tile([P, T], F32, name="y2")

@@ -78,10 +78,14 @@ def tile_moe_pre_lin_none_kernel(tc, xT, w_words, w_scales, gate, offs, pos1, po
         rounded = {}
         sums = {}
 
-        def gather(i):
+        staged = {}
+
+        def gather(i, rows=range(PACK)):
             a, s0, n = STEPS[i]
-            gated = stage.tile([P, PACK, n], F32, name="gated", tag="gated")
-            for r in range(PACK):
+            if i not in staged:
+                staged[i] = stage.tile([P, PACK, n], F32, name="gated", tag="gated")
+            gated = staged[i]
+            for r in rows:
                 cuts = [0, HEAD, n] if (i, r) == (0, 0) else [0, n]
                 for c0, c1 in zip(cuts, cuts[1:]):
                     nc.vector.tensor_tensor(
@@ -90,6 +94,8 @@ def tile_moe_pre_lin_none_kernel(tc, xT, w_words, w_scales, gate, offs, pos1, po
                         gates[:, s0 + c0 : s0 + c1],
                         MULT,
                     )
+            if PACK - 1 not in rows:
+                return
             h0 = s0 - s0 % HALF
             if (a, h0) not in rounded:
                 rounded[(a, h0)] = stage.tile([P, HALF, PACK], BF16, name="rounded", tag="rounded", align_bytes=64)
@@ -108,7 +114,7 @@ def tile_moe_pre_lin_none_kernel(tc, xT, w_words, w_scales, gate, offs, pos1, po
 
         def multiply(s0, n, passes):
             if s0 not in sums:
-                sums[s0] = psum.tile([P, n], F32, name="sums_%d" % s0)
+                sums[s0] = psum.tile([P, n], F32, name="sums", tag="bank_%d" % (len(sums) % 8))
             for e in range(s0 // C, (s0 + n) // C):
                 cols = slice(e * C, (e + 1) * C)
                 for a in passes:
@@ -126,7 +132,7 @@ def tile_moe_pre_lin_none_kernel(tc, xT, w_words, w_scales, gate, offs, pos1, po
             nc.scalar.copy(out=y[:, s0 : s0 + n], in_=sums[s0][:])
 
         every = range(PASSES)
-        late = range(HALF + BANK, S, C)
+        late = range(HALF, S, C)
         gather(0)
         gather(1)
         quantize(0, 0, HALF)
@@ -140,24 +146,30 @@ def tile_moe_pre_lin_none_kernel(tc, xT, w_words, w_scales, gate, offs, pos1, po
         copy_out(0, BANK)
         copy_out(BANK, BANK)
         quantize(0, HALF, HALF)
-        gather(5)
+        for s0 in late:
+            multiply(s0, C, [0])
+        gather(5, [0, 1, 2])
         quantize(1, HALF, HALF)
         for s0 in late:
-            multiply(s0, C, [0, 1])
-        gather(6)
+            multiply(s0, C, [1])
+        gather(5, [3])
+        gather(6, [0, 1, 2])
         quantize(2, HALF, BANK)
-        multiply(HALF, BANK, every)
-        gather(7)
-        copy_out(HALF, BANK)
-        quantize(2, 1536, 256)
-        multiply(1536, C, [2])
-        multiply(1664, C, [2])
-        quantize(2, 1792, 128)
-        multiply(1792, C, [2])
-        quantize(2, 1920, 128)
-        multiply(1920, C, [2])
-        for s0 in late:
+        quantize(2, late[4], C)
+        for s0 in late[:5]:
+            multiply(s0, C, [2])
+        gather(6, [3])
+        for s0 in late[:5]:
             copy_out(s0, C)
+        gather(7)
+        quantize(2, late[5], 2 * C)
+        multiply(late[5], C, [2])
+        multiply(late[6], C, [2])
+        quantize(2, late[7], C)
+        multiply(late[7], C, [2])
+        for s0 in late[5:7]:
+            nc.vector.tensor_copy(out=y[:, s0 : s0 + C], in_=sums[s0][:])
+        copy_out(late[7], C)
 
         y1 = keep.tile([P, T], F32, name="y1")
         y2 = keep.tile([P, T], F32, name="y2")
@@ -166,14 +178,12 @@ def tile_moe_pre_lin_none_kernel(tc, xT, w_words, w_scales, gate, offs, pos1, po
         def fetch(dst, slots, t0, t1):
             nc.vector.tensor_copy(dst[:, t0:t1], y[:].indirect(slots[:, t0 // GROUP : t1 // GROUP]))
 
-        def combine(t0, t1):
-            nc.vector.tensor_tensor(total[:, t0:t1], y1[:, t0:t1], y2[:, t0:t1], ADD)
+        def combine(engine, t0, t1):
+            engine.tensor_tensor(total[:, t0:t1], y1[:, t0:t1], y2[:, t0:t1], ADD)
             nc.sync.dma_start(out=out[:, t0:t1], in_=total[:, t0:t1])
 
-        cut = T - TAIL
-        fetch(y1, first_slots, 0, cut)
-        fetch(y2, second_slots, 0, cut)
-        fetch(y1, first_slots, cut, T)
-        combine(0, cut)
-        fetch(y2, second_slots, cut, T)
-        combine(cut, T)
+        cuts = [0, 512, 768, T]
+        for t0, t1 in zip(cuts, cuts[1:]):
+            fetch(y1, first_slots, t0, t1)
+            fetch(y2, second_slots, t0, t1)
+            combine(nc.vector if t1 == T else nc.gpsimd, t0, t1)

@@ -29,7 +29,7 @@ TAIL = 256
 BANK = 512
 
 STEPS = [(0, 0, 1024), (1, 0, 1024), (2, 0, 1024), (0, 1024, 1024), (1, 1024, 1024),
-         (2, 1024, 640), (2, 1664, 256), (2, 1920, 128)]
+         (2, 1024, 512), (2, 1536, 384), (2, 1920, 128)]
 
 
 def tile_moe_pre_lin_none_kernel(tc, xT, w_words, w_scales, gate, offs, pos1, pos2, out):
@@ -83,7 +83,7 @@ def tile_moe_pre_lin_none_kernel(tc, xT, w_words, w_scales, gate, offs, pos1, po
         def gather(i, rows=range(PACK)):
             a, s0, n = STEPS[i]
             if i not in staged:
-                staged[i] = stage.tile([P, PACK, n], F32, name="gated", tag="gated")
+                staged[i] = stage.tile([P, PACK, n], F32, name="gated", tag="gated", bufs=2)
             gated = staged[i]
             for r in rows:
                 cuts = [0, HEAD, n] if (i, r) == (0, 0) else [0, n]
@@ -148,27 +148,26 @@ def tile_moe_pre_lin_none_kernel(tc, xT, w_words, w_scales, gate, offs, pos1, po
         quantize(0, HALF, HALF)
         for s0 in late:
             multiply(s0, C, [0])
-        gather(5, [0, 1, 2])
+        gather(5)
         quantize(1, HALF, HALF)
         for s0 in late:
             multiply(s0, C, [1])
-        gather(5, [3])
-        gather(6, [0, 1, 2])
+        gather(6)
         quantize(2, HALF, BANK)
-        quantize(2, late[4], C)
-        for s0 in late[:5]:
+        for s0 in late[:4]:
             multiply(s0, C, [2])
-        gather(6, [3])
-        for s0 in late[:5]:
-            copy_out(s0, C)
         gather(7)
-        quantize(2, late[5], 2 * C)
+        quantize(2, late[4], 2 * C)
+        multiply(late[4], C, [2])
         multiply(late[5], C, [2])
+        quantize(2, late[6], C)
         multiply(late[6], C, [2])
         quantize(2, late[7], C)
         multiply(late[7], C, [2])
-        for s0 in late[5:7]:
+        for s0 in late[4:7]:
             nc.vector.tensor_copy(out=y[:, s0 : s0 + C], in_=sums[s0][:])
+        for s0 in late[:4]:
+            copy_out(s0, C)
         copy_out(late[7], C)
 
         y1 = keep.tile([P, T], F32, name="y1")

@@ -24,7 +24,7 @@ PASSES = K // (P * PACK)
 GROUP = 16
 PAD = 16
 HALF = S // 2
-HEAD = 320
+HEAD = [0, 128, 416, 1024]
 TAIL = 256
 BANK = 512
 
@@ -58,8 +58,8 @@ def tile_moe_pre_lin_none_kernel(tc, xT, w_words, w_scales, gate, offs, pos1, po
         x_view = xT.rearrange("(a p r) t -> a r p t", p=P, r=PACK)
         nc.sync.dma_start(out=x_rows[0][0][:, :T], in_=x_view[0, 0])
         nc.sync.dma_start(slot_tokens[:], offs)
-        nc.sync.dma_start(out=gates[:, :HEAD], in_=gate[:P, :HEAD])
-        nc.sync.dma_start(out=gates[:, HEAD:HALF], in_=gate[:P, HEAD:HALF])
+        for c0, c1 in zip(HEAD, HEAD[1:]):
+            nc.sync.dma_start(out=gates[:, c0:c1], in_=gate[:P, c0:c1])
         for a in range(PASSES):
             for r in range(PACK):
                 if (a, r) != (0, 0):
@@ -86,7 +86,7 @@ def tile_moe_pre_lin_none_kernel(tc, xT, w_words, w_scales, gate, offs, pos1, po
                 staged[i] = stage.tile([P, PACK, n], F32, name="gated", tag="gated", bufs=2)
             gated = staged[i]
             for r in rows:
-                cuts = [0, HEAD, n] if (i, r) == (0, 0) else [0, n]
+                cuts = HEAD if (i, r) == (0, 0) else [0, n]
                 for c0, c1 in zip(cuts, cuts[1:]):
                     nc.vector.tensor_tensor(
                         gated[:, r, c0:c1],

@@ -23,166 +23,163 @@ PACK = 4
 PASSES = K // (P * PACK)
 GROUP = 16
 PAD = 16
-HALF = S // 2
-HEAD = [0, 128, 416, 1024]
-TAIL = 256
 BANK = 512
+EARLY = 1280
+HEAD = [0, 128, 416, 1088, S]
 
-STEPS = [(0, 0, 1024), (1, 0, 1024), (2, 0, 1024), (0, 1024, 1024), (1, 1024, 1024),
-         (2, 1024, 512), (2, 1536, 384), (2, 1920, 128)]
+STEPS = [(0, 0, S), (1, 0, EARLY), (2, 0, EARLY), (1, EARLY, S), (2, EARLY, 1792), (2, 1792, 1984), (2, 1984, S)]
 
 
 def tile_moe_pre_lin_none_kernel(tc, xT, w_words, w_scales, gate, offs, pos1, pos2, out):
     nc = tc.nc
     with ExitStack() as ctx:
         keep = ctx.enter_context(tc.tile_pool(name="keep", bufs=1))
-        stage = ctx.enter_context(tc.tile_pool(name="stage", bufs=3))
+        stage = ctx.enter_context(tc.tile_pool(name="stage", bufs=1))
         psum = ctx.enter_context(tc.psum_pool(name="psum", bufs=1))
 
         slot_tokens = keep.tile([P, S // GROUP], U16, name="slot_tokens")
         first_slots = keep.tile([P, T // GROUP], U16, name="first_slots")
         second_slots = keep.tile([P, T // GROUP], U16, name="second_slots")
-        x_rows = [[keep.tile([P, T + PAD], F32, name="x_rows_%d_%d" % (a, r)) for r in range(PACK)] for a in range(PASSES)]
+        wide = [keep.tile([P, S + PAD], F32, name="wide_%d" % r) for r in range(PACK)]
+        narrow = [[keep.tile([P, EARLY + PAD], F32, name="narrow_%d_%d" % (a, r)) for r in range(PACK)] for a in (1, 2)]
+        x_rows = [wide] + narrow
         gates = keep.tile([P, S], F32, name="gates")
         w_codes = keep.tile([P, E * PASSES, N], U32, name="w_codes", align_bytes=64)
-        w_plane = keep.tile([P, E * PASSES, N], U8, name="w_plane", align_bytes=64)
+        w_plane = keep.tile([P, E, N], U8, name="w_plane", align_bytes=64)
         x_codes = keep.tile([P, PASSES, S], U32, name="x_codes", align_bytes=64)
         x_plane = keep.tile([P, PASSES, S], U8, name="x_plane", align_bytes=64)
         y = keep.tile([P, S], F32, name="y")
 
-        for a in range(PASSES):
-            for r in range(PACK):
-                nc.vector.memset(x_rows[a][r][:, T:], 0.0)
-        nc.vector.memset(w_plane[:].bitcast(I32), 0)
+        for r in range(PACK):
+            (nc.vector if r < 2 else nc.gpsimd).memset(wide[r][:, T:].bitcast(I32), 0)
+        for rows in narrow:
+            for row in rows:
+                nc.gpsimd.memset(row[:, T:].bitcast(I32), 0)
+        nc.gpsimd.memset(w_plane[:].bitcast(I32), 0)
 
         x_view = xT.rearrange("(a p r) t -> a r p t", p=P, r=PACK)
-        nc.sync.dma_start(out=x_rows[0][0][:, :T], in_=x_view[0, 0])
+
+        def load_rows(a, rows):
+            for r in rows:
+                nc.sync.dma_start(out=x_rows[a][r][:, :T], in_=x_view[a, r])
+
+        load_rows(0, [0])
         nc.sync.dma_start(slot_tokens[:], offs)
         for c0, c1 in zip(HEAD, HEAD[1:]):
             nc.sync.dma_start(out=gates[:, c0:c1], in_=gate[:P, c0:c1])
-        for a in range(PASSES):
-            for r in range(PACK):
-                if (a, r) != (0, 0):
-                    nc.sync.dma_start(out=x_rows[a][r][:, :T], in_=x_view[a, r])
-        nc.sync.dma_start(out=gates[:, HALF:], in_=gate[:P, HALF:])
-        scale_rows = w_scales.rearrange("e a q n -> q (e a) n")
+        load_rows(0, range(1, PACK))
+        load_rows(1, range(PACK))
+        load_rows(2, range(PACK))
+        scale_rows = w_scales.rearrange("e a q n -> a q e n")
         for quad in range(4):
-            nc.sync.dma_start(out=w_plane[32 * quad : 32 * quad + 4].bitcast(I32),
-                              in_=scale_rows[4 * quad : 4 * quad + 4].bitcast(I32))
+            for a in range(PASSES):
+                nc.sync.dma_start(out=w_plane[32 * quad + 4 * a : 32 * quad + 4 * a + 4].bitcast(I32),
+                                  in_=scale_rows[a, 4 * quad : 4 * quad + 4].bitcast(I32))
         word_rows = w_words.rearrange("e a p n r -> p (e a) (n r)").bitcast(I32)
-        for j0 in range(0, E * PASSES, 4 * PASSES):
-            nc.sync.dma_start(out=w_codes[:, j0 : j0 + 4 * PASSES, :].bitcast(I32), in_=word_rows[:, j0 : j0 + 4 * PASSES, :])
-        nc.sync.dma_start(first_slots[:], pos1)
-        nc.sync.dma_start(second_slots[:], pos2)
+
+        def load_words(e0, e1):
+            nc.sync.dma_start(out=w_codes[:, e0 * PASSES : e1 * PASSES, :].bitcast(I32), in_=word_rows[:, e0 * PASSES : e1 * PASSES, :])
 
         rounded = {}
         sums = {}
 
-        staged = {}
-
-        def gather(i, rows=range(PACK)):
-            a, s0, n = STEPS[i]
-            if i not in staged:
-                staged[i] = stage.tile([P, PACK, n], F32, name="gated", tag="gated", bufs=2)
-            gated = staged[i]
-            for r in rows:
-                cuts = HEAD if (i, r) == (0, 0) else [0, n]
+        def gather(i):
+            a, s0, s1 = STEPS[i]
+            gated = stage.tile([P, PACK, s1 - s0], F32, name="gated", tag="gated_%d" % (i % 2))
+            for r in range(PACK):
+                cuts = HEAD if (i, r) == (0, 0) else [s0, s1]
                 for c0, c1 in zip(cuts, cuts[1:]):
                     nc.vector.tensor_tensor(
-                        gated[:, r, c0:c1],
-                        x_rows[a][r][:].indirect(slot_tokens[:, (s0 + c0) // GROUP : (s0 + c1) // GROUP]),
-                        gates[:, s0 + c0 : s0 + c1],
+                        gated[:, r, c0 - s0 : c1 - s0],
+                        x_rows[a][r][:].indirect(slot_tokens[:, c0 // GROUP : c1 // GROUP]),
+                        gates[:, c0:c1],
                         MULT,
                     )
-            if PACK - 1 not in rows:
-                return
-            h0 = s0 - s0 % HALF
-            if (a, h0) not in rounded:
-                rounded[(a, h0)] = stage.tile([P, HALF, PACK], BF16, name="rounded", tag="rounded", align_bytes=64)
-            nc.scalar.copy(
-                out=rounded[(a, h0)][:, s0 - h0 : s0 - h0 + n, :].rearrange("p (c i) r -> p c r i", i=4),
-                in_=gated[:].rearrange("p r (c i) -> p c r i", i=4),
-            )
+            if a not in rounded:
+                rounded[a] = stage.tile([P, S, PACK], BF16, name="rounded", tag="rounded_%d" % (a % 2), align_bytes=64)
+            for c0 in range(s0, s1, 1024):
+                c1 = min(c0 + 1024, s1)
+                nc.scalar.copy(
+                    out=rounded[a][:, c0:c1, :].rearrange("p (c i) r -> p c r i", i=4),
+                    in_=gated[:, :, c0 - s0 : c1 - s0].rearrange("p r (c i) -> p c r i", i=4),
+                )
 
-        def quantize(a, s0, n):
-            h0 = s0 - s0 % HALF
+        def quantize(a, s0, s1):
             nc.vector.quantize_mx(
-                out=x_codes[:, a, s0 : s0 + n].bitcast(FP8X4),
-                scales=x_plane[:, a, s0 : s0 + n],
-                in_=rounded[(a, h0)][:, s0 - h0 : s0 - h0 + n, :].rearrange("p n r -> p (n r)"),
+                out=x_codes[:, a, s0:s1].bitcast(FP8X4),
+                scales=x_plane[:, a, s0:s1],
+                in_=rounded[a][:, s0:s1, :].rearrange("p n r -> p (n r)"),
             )
 
-        def multiply(s0, n, passes):
-            if s0 not in sums:
-                sums[s0] = psum.tile([P, n], F32, name="sums", tag="bank_%d" % (len(sums) % 8))
-            for e in range(s0 // C, (s0 + n) // C):
+        def multiply(e0, e1, bank, passes):
+            if e0 not in sums:
+                sums[e0] = psum.tile([P, (e1 - e0) * C], F32, name="sums", tag="bank_%d" % bank)
+            for e in range(e0, e1):
                 cols = slice(e * C, (e + 1) * C)
                 for a in passes:
                     nc.tensor.matmul_mx(
-                        out=sums[s0][:, e * C - s0 : (e + 1) * C - s0],
+                        out=sums[e0][:, (e - e0) * C : (e - e0 + 1) * C],
                         lhsT=w_codes[:, e * PASSES + a, :].bitcast(FP8X4),
-                        lhsT_scale=w_plane[:, e * PASSES + a, :],
+                        lhsT_scale=w_plane[4 * a :, e, :],
                         rhs=x_codes[:, a, cols].bitcast(FP8X4),
                         rhs_scale=x_plane[:, a, cols],
                         start=(a == 0),
                         stop=(a == PASSES - 1),
                     )
 
-        def copy_out(s0, n):
-            nc.scalar.copy(out=y[:, s0 : s0 + n], in_=sums[s0][:])
+        def copy_out(engine_copy, e0, e1):
+            engine_copy(out=y[:, e0 * C : e1 * C], in_=sums[e0][:])
 
         every = range(PASSES)
-        late = range(HALF, S, C)
+        late = range(EARLY // C, E)
+        late_bank = {e: (3 + e - late[0]) % 8 for e in late}
         gather(0)
+        for e0 in range(0, E, 4):
+            load_words(e0, e0 + 4)
+        nc.sync.dma_start(first_slots[:], pos1)
+        nc.sync.dma_start(second_slots[:], pos2)
         gather(1)
-        quantize(0, 0, HALF)
+        quantize(0, 0, 1024)
+        quantize(0, 1024, S)
+        for e in late[:-1]:
+            multiply(e, e + 1, late_bank[e], [0])
         gather(2)
-        quantize(1, 0, HALF)
+        quantize(1, 0, 1024)
         gather(3)
-        quantize(2, 0, HALF)
-        multiply(0, BANK, every)
-        multiply(BANK, BANK, every)
+        quantize(2, 0, 1024)
+        quantize(2, 1024, EARLY)
+        multiply(0, 4, 0, every)
+        multiply(4, 8, 1, every)
+        copy_out(nc.scalar.copy, 0, 4)
+        copy_out(nc.scalar.copy, 4, 8)
+        multiply(E - 1, E, late_bank[E - 1], [0])
         gather(4)
-        copy_out(0, BANK)
-        copy_out(BANK, BANK)
-        quantize(0, HALF, HALF)
-        for s0 in late:
-            multiply(s0, C, [0])
+        quantize(1, 1024, S)
+        multiply(8, 10, 2, every)
+        for e in late:
+            multiply(e, e + 1, late_bank[e], [1])
+        copy_out(nc.scalar.copy, 8, 10)
         gather(5)
-        quantize(1, HALF, HALF)
-        for s0 in late:
-            multiply(s0, C, [1])
+        quantize(2, EARLY, 1536)
+        for e in (10, 11):
+            multiply(e, e + 1, late_bank[e], [2])
         gather(6)
-        quantize(2, HALF, BANK)
-        for s0 in late[:4]:
-            multiply(s0, C, [2])
-        gather(7)
-        quantize(2, late[4], 2 * C)
-        multiply(late[4], C, [2])
-        multiply(late[5], C, [2])
-        quantize(2, late[6], C)
-        multiply(late[6], C, [2])
-        quantize(2, late[7], C)
-        multiply(late[7], C, [2])
-        for s0 in late[4:7]:
-            nc.vector.tensor_copy(out=y[:, s0 : s0 + C], in_=sums[s0][:])
-        for s0 in late[:4]:
-            copy_out(s0, C)
-        copy_out(late[7], C)
+        quantize(2, 1536, 1792)
+        for e in (12, 13):
+            multiply(e, e + 1, late_bank[e], [2])
+        quantize(2, 1792, 1920)
+        multiply(14, 15, late_bank[14], [2])
+        quantize(2, 1920, S)
+        multiply(15, 16, late_bank[15], [2])
+        for e in late[:-1]:
+            copy_out(nc.scalar.copy, e, e + 1)
+        copy_out(nc.vector.tensor_copy, 15, 16)
 
-        y1 = keep.tile([P, T], F32, name="y1")
-        y2 = keep.tile([P, T], F32, name="y2")
-        total = keep.tile([P, T], F32, name="total")
+        y1 = stage.tile([P, T], F32, name="y1", tag="gated_1")
+        total = stage.tile([P, T], F32, name="total", tag="gated_0")
 
-        def fetch(dst, slots, t0, t1):
-            nc.vector.tensor_copy(dst[:, t0:t1], y[:].indirect(slots[:, t0 // GROUP : t1 // GROUP]))
-
-        def combine(engine, t0, t1):
-            engine.tensor_tensor(total[:, t0:t1], y1[:, t0:t1], y2[:, t0:t1], ADD)
+        for t0, t1 in ((0, 640), (640, T)):
+            nc.vector.tensor_copy(y1[:, t0:t1], y[:].indirect(first_slots[:, t0 // GROUP : t1 // GROUP]))
+        for t0, t1 in ((0, 640), (640, 896), (896, T)):
+            nc.vector.tensor_tensor(total[:, t0:t1], y[:].indirect(second_slots[:, t0 // GROUP : t1 // GROUP]), y1[:, t0:t1], ADD)
             nc.sync.dma_start(out=out[:, t0:t1], in_=total[:, t0:t1])
-
-        cuts = [0, 512, 768, T]
-        for t0, t1 in zip(cuts, cuts[1:]):
-            fetch(y1, first_slots, t0, t1)
-            fetch(y2, second_slots, t0, t1)
-            combine(nc.vector if t1 == T else nc.gpsimd, t0, t1)

@@ -50,12 +50,7 @@ def tile_moe_pre_lin_none_kernel(tc, xT, w_words, w_scales, gate, offs, pos1, po
         x_plane = keep.tile([P, PASSES, S], U8, name="x_plane", align_bytes=64)
         y = keep.tile([P, S], F32, name="y")
 
-        for r in range(PACK):
-            (nc.vector if r < 2 else nc.gpsimd).memset(wide[r][:, T:].bitcast(I32), 0)
-        for rows in narrow:
-            for row in rows:
-                nc.gpsimd.memset(row[:, T:].bitcast(I32), 0)
-        nc.gpsimd.memset(w_plane[:].bitcast(I32), 0)
+        nc.vector.memset(w_plane[:].bitcast(I32), 0)
 
         x_view = xT.rearrange("(a p r) t -> a r p t", p=P, r=PACK)
 

@@ -27,7 +27,7 @@ BANK = 512
 EARLY = 1280
 HEAD = [0, 128, 416, 1088, S]
 
-STEPS = [(0, 0, S), (1, 0, EARLY), (2, 0, EARLY), (1, EARLY, S), (2, EARLY, 1792), (2, 1792, 1984), (2, 1984, S)]
+STEPS = [(0, 0, S), (1, 0, S), (2, 0, EARLY), (2, EARLY, 1792), (2, 1792, 1984), (2, 1984, S)]
 
 
 def tile_moe_pre_lin_none_kernel(tc, xT, w_words, w_scales, gate, offs, pos1, pos2, out):
@@ -40,9 +40,9 @@ def tile_moe_pre_lin_none_kernel(tc, xT, w_words, w_scales, gate, offs, pos1, po
         slot_tokens = keep.tile([P, S // GROUP], U16, name="slot_tokens")
         first_slots = keep.tile([P, T // GROUP], U16, name="first_slots")
         second_slots = keep.tile([P, T // GROUP], U16, name="second_slots")
-        wide = [keep.tile([P, S + PAD], F32, name="wide_%d" % r) for r in range(PACK)]
-        narrow = [[keep.tile([P, EARLY + PAD], F32, name="narrow_%d_%d" % (a, r)) for r in range(PACK)] for a in (1, 2)]
-        x_rows = [wide] + narrow
+        wide = [keep.tile([P, S + PAD], F32, name="wide_%d" % r) for r in range(6)]
+        narrow = [keep.tile([P, EARLY + PAD], F32, name="narrow_%d" % r) for r in range(PACK)]
+        x_rows = [wide[:4], wide[4:] + wide[:2], narrow]
         gates = keep.tile([P, S], F32, name="gates")
         w_codes = keep.tile([P, E * PASSES, N], U32, name="w_codes", align_bytes=64)
         w_plane = keep.tile([P, E, N], U8, name="w_plane", align_bytes=64)
@@ -63,13 +63,6 @@ def tile_moe_pre_lin_none_kernel(tc, xT, w_words, w_scales, gate, offs, pos1, po
         for c0, c1 in zip(HEAD, HEAD[1:]):
             nc.sync.dma_start(out=gates[:, c0:c1], in_=gate[:P, c0:c1])
         load_rows(0, range(1, PACK))
-        load_rows(1, range(PACK))
-        load_rows(2, range(PACK))
-        scale_rows = w_scales.rearrange("e a q n -> a q e n")
-        for quad in range(4):
-            for a in range(PASSES):
-                nc.sync.dma_start(out=w_plane[32 * quad + 4 * a : 32 * quad + 4 * a + 4].bitcast(I32),
-                                  in_=scale_rows[a, 4 * quad : 4 * quad + 4].bitcast(I32))
         word_rows = w_words.rearrange("e a p n r -> p (e a) (n r)").bitcast(I32)
 
         def load_words(e0, e1):
@@ -106,10 +99,10 @@ def tile_moe_pre_lin_none_kernel(tc, xT, w_words, w_scales, gate, offs, pos1, po
                 in_=rounded[a][:, s0:s1, :].rearrange("p n r -> p (n r)"),
             )
 
-        def multiply(e0, e1, bank, passes):
+        def multiply(e0, e1, bank, passes, experts=None):
             if e0 not in sums:
                 sums[e0] = psum.tile([P, (e1 - e0) * C], F32, name="sums", tag="bank_%d" % bank)
-            for e in range(e0, e1):
+            for e in experts or range(e0, e1):
                 cols = slice(e * C, (e + 1) * C)
                 for a in passes:
                     nc.tensor.matmul_mx(
@@ -122,13 +115,20 @@ def tile_moe_pre_lin_none_kernel(tc, xT, w_words, w_scales, gate, offs, pos1, po
                         stop=(a == PASSES - 1),
                     )
 
-        def copy_out(engine_copy, e0, e1):
-            engine_copy(out=y[:, e0 * C : e1 * C], in_=sums[e0][:])
+        def copy_out(engine_copy, e0, e1, first=None):
+            first = e0 if first is None else first
+            engine_copy(out=y[:, e0 * C : e1 * C], in_=sums[first][:, (e0 - first) * C : (e1 - first) * C])
 
         every = range(PASSES)
-        late = range(EARLY // C, E)
-        late_bank = {e: (3 + e - late[0]) % 8 for e in late}
+        late = range(11, E)
         gather(0)
+        load_rows(1, range(PACK))
+        load_rows(2, range(PACK))
+        scale_rows = w_scales.rearrange("e a q n -> a q e n")
+        for quad in range(4):
+            for a in range(PASSES):
+                nc.sync.dma_start(out=w_plane[32 * quad + 4 * a : 32 * quad + 4 * a + 4].bitcast(I32),
+                                  in_=scale_rows[a, 4 * quad : 4 * quad + 4].bitcast(I32))
         for e0 in range(0, E, 4):
             load_words(e0, e0 + 4)
         nc.sync.dma_start(first_slots[:], pos1)
@@ -136,42 +136,40 @@ def tile_moe_pre_lin_none_kernel(tc, xT, w_words, w_scales, gate, offs, pos1, po
         gather(1)
         quantize(0, 0, 1024)
         quantize(0, 1024, S)
-        for e in late[:-1]:
-            multiply(e, e + 1, late_bank[e], [0])
         gather(2)
         quantize(1, 0, 1024)
+        quantize(1, 1024, S)
+        for e in late:
+            multiply(e, e + 1, e - 8, [0, 1])
         gather(3)
         quantize(2, 0, 1024)
         quantize(2, 1024, EARLY)
         multiply(0, 4, 0, every)
         multiply(4, 8, 1, every)
+        multiply(8, 11, 2, every, range(8, 10))
         copy_out(nc.scalar.copy, 0, 4)
-        copy_out(nc.scalar.copy, 4, 8)
-        multiply(E - 1, E, late_bank[E - 1], [0])
         gather(4)
-        quantize(1, 1024, S)
-        multiply(8, 10, 2, every)
-        for e in late:
-            multiply(e, e + 1, late_bank[e], [1])
-        copy_out(nc.scalar.copy, 8, 10)
-        gather(5)
         quantize(2, EARLY, 1536)
-        for e in (10, 11):
-            multiply(e, e + 1, late_bank[e], [2])
-        gather(6)
+        multiply(8, 11, 2, every, range(10, 11))
+        multiply(11, 12, 3, [2])
+        copy_out(nc.scalar.copy, 4, 6)
+        gather(5)
         quantize(2, 1536, 1792)
         for e in (12, 13):
-            multiply(e, e + 1, late_bank[e], [2])
+            multiply(e, e + 1, e - 8, [2])
         quantize(2, 1792, 1920)
-        multiply(14, 15, late_bank[14], [2])
-        quantize(2, 1920, S)
-        multiply(15, 16, late_bank[15], [2])
+        multiply(14, 15, 6, [2])
+        quantize(2, 1920, 1984)
+        quantize(2, 1984, S)
+        multiply(15, 16, 7, [2])
+        copy_out(nc.scalar.copy, 6, 8, 4)
+        copy_out(nc.vector.tensor_copy, 8, 11)
         for e in late[:-1]:
             copy_out(nc.scalar.copy, e, e + 1)
         copy_out(nc.vector.tensor_copy, 15, 16)
 
-        y1 = stage.tile([P, T], F32, name="y1", tag="gated_1")
-        total = stage.tile([P, T], F32, name="total", tag="gated_0")
+        y1 = stage.tile([P, T], F32, name="y1", tag="gated_0")
+        total = stage.tile([P, T], F32, name="total", tag="gated_1")
 
         for t0, t1 in ((0, 640), (640, T)):
             nc.vector.tensor_copy(y1[:, t0:t1], y[:].indirect(first_slots[:, t0 // GROUP : t1 // GROUP]))

@@ -25,7 +25,7 @@ GROUP = 16
 PAD = 16
 BANK = 512
 EARLY = 1280
-HEAD = [0, 128, 416, 1088, S]
+HEAD = [0, 128, 352, 768, 1408, S]
 
 STEPS = [(0, 0, S), (1, 0, S), (2, 0, EARLY), (2, EARLY, 1792), (2, 1792, 1984), (2, 1984, S)]
 
@@ -164,9 +164,8 @@ def tile_moe_pre_lin_none_kernel(tc, xT, w_words, w_scales, gate, offs, pos1, po
         multiply(15, 16, 7, [2])
         copy_out(nc.scalar.copy, 6, 8, 4)
         copy_out(nc.vector.tensor_copy, 8, 11)
-        for e in late[:-1]:
-            copy_out(nc.scalar.copy, e, e + 1)
-        copy_out(nc.vector.tensor_copy, 15, 16)
+        for e in late:
+            copy_out(nc.vector.tensor_copy if e == 14 else nc.scalar.copy, e, e + 1)
 
         y1 = stage.tile([P, T], F32, name="y1", tag="gated_0")
         total = stage.tile([P, T], F32, name="total", tag="gated_1")

@@ -25,9 +25,11 @@ GROUP = 16
 PAD = 16
 BANK = 512
 EARLY = 1280
+LAST = S - 2 * C
 HEAD = [0, 128, 352, 768, 1408, S]
 
-STEPS = [(0, 0, S), (1, 0, S), (2, 0, EARLY), (2, EARLY, 1792), (2, 1792, 1984), (2, 1984, S)]
+STEPS = [(0, 0, S), (1, 0, S), (2, 0, EARLY), (2, EARLY, S)]
+BANKS = [(0, 4), (4, 8), (8, 12), (12, 14), (14, 15), (15, 16)]
 
 
 def tile_moe_pre_lin_none_kernel(tc, xT, w_words, w_scales, gate, offs, pos1, pos2, out):
@@ -41,14 +43,15 @@ def tile_moe_pre_lin_none_kernel(tc, xT, w_words, w_scales, gate, offs, pos1, po
         first_slots = keep.tile([P, T // GROUP], U16, name="first_slots")
         second_slots = keep.tile([P, T // GROUP], U16, name="second_slots")
         wide = [keep.tile([P, S + PAD], F32, name="wide_%d" % r) for r in range(6)]
-        narrow = [keep.tile([P, EARLY + PAD], F32, name="narrow_%d" % r) for r in range(PACK)]
+        narrow = [keep.tile([P, EARLY + PAD], F32, name="narrow_%d" % r) for r in range(PACK - 1)]
+        narrow = narrow[:2] + [stage.tile([P, S], F32, name="last_row", tag="last_row", align_bytes=64)] + narrow[2:]
         x_rows = [wide[:4], wide[4:] + wide[:2], narrow]
         gates = keep.tile([P, S], F32, name="gates")
         w_codes = keep.tile([P, E * PASSES, N], U32, name="w_codes", align_bytes=64)
         w_plane = keep.tile([P, E, N], U8, name="w_plane", align_bytes=64)
-        x_codes = keep.tile([P, PASSES, S], U32, name="x_codes", align_bytes=64)
+        x_codes = {a: keep.tile([P, S], U32, name="x_codes_%d" % a, align_bytes=64) for a in (0, 2)}
         x_plane = keep.tile([P, PASSES, S], U8, name="x_plane", align_bytes=64)
-        y = keep.tile([P, S], F32, name="y")
+        y = keep.tile([P, S], F32, name="y", align_bytes=64)
 
         nc.vector.memset(w_plane[:].bitcast(I32), 0)
 
@@ -70,6 +73,14 @@ def tile_moe_pre_lin_none_kernel(tc, xT, w_words, w_scales, gate, offs, pos1, po
 
         rounded = {}
         sums = {}
+        done = [0] * len(BANKS)
+
+        last_rounded = y[:, 1536:S].bitcast(BF16).rearrange("p (n r) -> p n r", r=PACK)
+
+        def rounded_slots(a, s0, s1):
+            if a == PASSES - 1 and s0 >= LAST:
+                return last_rounded[:, s0 - LAST : s1 - LAST, :]
+            return rounded[a][:, s0:s1, :]
 
         def gather(i):
             a, s0, s1 = STEPS[i]
@@ -85,45 +96,45 @@ def tile_moe_pre_lin_none_kernel(tc, xT, w_words, w_scales, gate, offs, pos1, po
                     )
             if a not in rounded:
                 rounded[a] = stage.tile([P, S, PACK], BF16, name="rounded", tag="rounded_%d" % (a % 2), align_bytes=64)
-            for c0 in range(s0, s1, 1024):
-                c1 = min(c0 + 1024, s1)
+            cuts = [s0, s0 + 1024, s1] if s1 - s0 > 1024 else [s0, 1536, LAST, s1]
+            for c0, c1 in zip(cuts, cuts[1:]):
                 nc.scalar.copy(
-                    out=rounded[a][:, c0:c1, :].rearrange("p (c i) r -> p c r i", i=4),
+                    out=rounded_slots(a, c0, c1).rearrange("p (c i) r -> p c r i", i=4),
                     in_=gated[:, :, c0 - s0 : c1 - s0].rearrange("p r (c i) -> p c r i", i=4),
                 )
 
         def quantize(a, s0, s1):
             nc.vector.quantize_mx(
-                out=x_codes[:, a, s0:s1].bitcast(FP8X4),
+                out=x_codes[a][:, s0:s1].bitcast(FP8X4),
                 scales=x_plane[:, a, s0:s1],
-                in_=rounded[a][:, s0:s1, :].rearrange("p n r -> p (n r)"),
+                in_=rounded_slots(a, s0, s1).rearrange("p n r -> p (n r)"),
             )
 
-        def multiply(e0, e1, bank, passes, experts=None):
-            if e0 not in sums:
-                sums[e0] = psum.tile([P, (e1 - e0) * C], F32, name="sums", tag="bank_%d" % bank)
-            for e in experts or range(e0, e1):
-                cols = slice(e * C, (e + 1) * C)
-                for a in passes:
+        def multiply(a, banks):
+            for b in banks:
+                e0, e1 = BANKS[b]
+                if b not in sums:
+                    sums[b] = psum.tile([P, (e1 - e0) * C], F32, name="sums", tag="bank_%d" % b)
+                for e in range(e0, e1):
+                    cols = slice(e * C, (e + 1) * C)
                     nc.tensor.matmul_mx(
-                        out=sums[e0][:, (e - e0) * C : (e - e0 + 1) * C],
+                        out=sums[b][:, (e - e0) * C : (e - e0 + 1) * C],
                         lhsT=w_codes[:, e * PASSES + a, :].bitcast(FP8X4),
                         lhsT_scale=w_plane[4 * a :, e, :],
-                        rhs=x_codes[:, a, cols].bitcast(FP8X4),
+                        rhs=x_codes[a][:, cols].bitcast(FP8X4),
                         rhs_scale=x_plane[:, a, cols],
-                        start=(a == 0),
-                        stop=(a == PASSES - 1),
+                        start=(done[b] == 0),
+                        stop=(done[b] == PASSES * (e1 - e0) - 1),
                     )
+                    done[b] += 1
 
-        def copy_out(engine_copy, e0, e1, first=None):
-            first = e0 if first is None else first
-            engine_copy(out=y[:, e0 * C : e1 * C], in_=sums[first][:, (e0 - first) * C : (e1 - first) * C])
+        def copy_out(engine_copy, b):
+            e0, e1 = BANKS[b]
+            engine_copy(out=y[:, e0 * C : e1 * C], in_=sums[b][:])
 
-        every = range(PASSES)
-        late = range(11, E)
+        every = range(len(BANKS))
         gather(0)
-        load_rows(1, range(PACK))
-        load_rows(2, range(PACK))
+        load_rows(1, range(2))
         scale_rows = w_scales.rearrange("e a q n -> a q e n")
         for quad in range(4):
             for a in range(PASSES):
@@ -131,41 +142,34 @@ def tile_moe_pre_lin_none_kernel(tc, xT, w_words, w_scales, gate, offs, pos1, po
                                   in_=scale_rows[a, 4 * quad : 4 * quad + 4].bitcast(I32))
         for e0 in range(0, E, 4):
             load_words(e0, e0 + 4)
+        load_rows(1, range(2, PACK))
+        load_rows(2, range(PACK))
         nc.sync.dma_start(first_slots[:], pos1)
         nc.sync.dma_start(second_slots[:], pos2)
         gather(1)
         quantize(0, 0, 1024)
         quantize(0, 1024, S)
+        multiply(0, every)
         gather(2)
-        quantize(1, 0, 1024)
-        quantize(1, 1024, S)
-        for e in late:
-            multiply(e, e + 1, e - 8, [0, 1])
         gather(3)
+        x_codes[1] = stage.tile([P, S], U32, name="x_codes_1", tag="last_row", align_bytes=64)
+        quantize(1, 0, 1024)
+        multiply(1, [0, 1])
         quantize(2, 0, 1024)
-        quantize(2, 1024, EARLY)
-        multiply(0, 4, 0, every)
-        multiply(4, 8, 1, every)
-        multiply(8, 11, 2, every, range(8, 10))
-        copy_out(nc.scalar.copy, 0, 4)
-        gather(4)
-        quantize(2, EARLY, 1536)
-        multiply(8, 11, 2, every, range(10, 11))
-        multiply(11, 12, 3, [2])
-        copy_out(nc.scalar.copy, 4, 6)
-        gather(5)
-        quantize(2, 1536, 1792)
-        for e in (12, 13):
-            multiply(e, e + 1, e - 8, [2])
-        quantize(2, 1792, 1920)
-        multiply(14, 15, 6, [2])
-        quantize(2, 1920, 1984)
-        quantize(2, 1984, S)
-        multiply(15, 16, 7, [2])
-        copy_out(nc.scalar.copy, 6, 8, 4)
-        copy_out(nc.vector.tensor_copy, 8, 11)
-        for e in late:
-            copy_out(nc.vector.tensor_copy if e == 14 else nc.scalar.copy, e, e + 1)
+        multiply(2, [0, 1])
+        quantize(1, 1024, 1536)
+        multiply(1, [2])
+        quantize(2, 1024, 1536)
+        multiply(2, [2])
+        quantize(1, 1536, S)
+        multiply(1, [3, 4, 5])
+        quantize(2, 1536, LAST)
+        multiply(2, [3])
+        quantize(2, LAST, S)
+        multiply(2, [4, 5])
+        for b in (0, 1, 2, 3, 5):
+            copy_out(nc.scalar.copy, b)
+        copy_out(nc.vector.tensor_copy, 4)
 
         y1 = stage.tile([P, T], F32, name="y1", tag="gated_0")
         total = stage.tile([P, T], F32, name="total", tag="gated_1")

@@ -24,7 +24,7 @@ PASSES = K // (P * PACK)
 GROUP = 16
 PAD = 16
 BANK = 512
-EARLY = 1280
+EARLY = 1344
 LAST = S - 2 * C
 HEAD = [0, 128, 352, 768, 1408, S]
 
@@ -167,9 +167,10 @@ def tile_moe_pre_lin_none_kernel(tc, xT, w_words, w_scales, gate, offs, pos1, po
         multiply(2, [3])
         quantize(2, LAST, S)
         multiply(2, [4, 5])
-        for b in (0, 1, 2, 3, 5):
+        for b in (0, 1, 2, 5):
             copy_out(nc.scalar.copy, b)
-        copy_out(nc.vector.tensor_copy, 4)
+        for b in (3, 4):
+            copy_out(nc.vector.tensor_copy, b)
 
         y1 = stage.tile([P, T], F32, name="y1", tag="gated_0")
         total = stage.tile([P, T], F32, name="total", tag="gated_1")

@@ -17,18 +17,17 @@ U8 = mybir.dt.uint8
 FP8X4 = mybir.dt.float8_e4m3fn_x4
 MULT = mybir.AluOpType.mult
 ADD = mybir.AluOpType.add
+COPY = mybir.ActivationFunctionType.Copy
 
 P = 128
 PACK = 4
 PASSES = K // (P * PACK)
 GROUP = 16
 PAD = 16
-BANK = 512
-EARLY = 1344
-LAST = S - 2 * C
-HEAD = [0, 128, 352, 768, 1408, S]
+RUN = 4
 
-STEPS = [(0, 0, S), (1, 0, S), (2, 0, EARLY), (2, EARLY, S)]
+OWN = {0: 448, 2: 1024}
+CUTS = [[448, 1024, S], [0, 1024, S], [1024, 1536, 1792, S]]
 BANKS = [(0, 4), (4, 8), (8, 12), (12, 14), (14, 15), (15, 16)]
 
 
@@ -42,14 +41,12 @@ def tile_moe_pre_lin_none_kernel(tc, xT, w_words, w_scales, gate, offs, pos1, po
         slot_tokens = keep.tile([P, S // GROUP], U16, name="slot_tokens")
         first_slots = keep.tile([P, T // GROUP], U16, name="first_slots")
         second_slots = keep.tile([P, T // GROUP], U16, name="second_slots")
-        wide = [keep.tile([P, S + PAD], F32, name="wide_%d" % r) for r in range(6)]
-        narrow = [keep.tile([P, EARLY + PAD], F32, name="narrow_%d" % r) for r in range(PACK - 1)]
-        narrow = narrow[:2] + [stage.tile([P, S], F32, name="last_row", tag="last_row", align_bytes=64)] + narrow[2:]
-        x_rows = [wide[:4], wide[4:] + wide[:2], narrow]
+        x_rows = [[keep.tile([P, T + PAD], F32, name="x_row_%d_%d" % (a, r)) for r in range(PACK)] for a in range(PASSES)]
         gates = keep.tile([P, S], F32, name="gates")
         w_codes = keep.tile([P, E * PASSES, N], U32, name="w_codes", align_bytes=64)
         w_plane = keep.tile([P, E, N], U8, name="w_plane", align_bytes=64)
-        x_codes = {a: keep.tile([P, S], U32, name="x_codes_%d" % a, align_bytes=64) for a in (0, 2)}
+        rounded = [keep.tile([P, S, PACK], BF16, name="rounded_%d" % a, align_bytes=64) for a in range(PASSES)]
+        x_codes = [keep.tile([P, S], U32, name="x_codes_%d" % a, align_bytes=64) for a in range(PASSES)]
         x_plane = keep.tile([P, PASSES, S], U8, name="x_plane", align_bytes=64)
         y = keep.tile([P, S], F32, name="y", align_bytes=64)
 
@@ -63,51 +60,59 @@ def tile_moe_pre_lin_none_kernel(tc, xT, w_words, w_scales, gate, offs, pos1, po
 
         load_rows(0, [0])
         nc.sync.dma_start(slot_tokens[:], offs)
-        for c0, c1 in zip(HEAD, HEAD[1:]):
-            nc.sync.dma_start(out=gates[:, c0:c1], in_=gate[:P, c0:c1])
+        nc.sync.dma_start(out=gates[:, : OWN[0]], in_=gate[:P, : OWN[0]])
         load_rows(0, range(1, PACK))
+        nc.sync.dma_start(out=gates[:, OWN[0] :], in_=gate[:P, OWN[0] :])
+        load_rows(2, range(2))
+        load_rows(1, range(PACK))
+        load_rows(2, range(2, PACK))
+        scale_rows = w_scales.rearrange("e a q n -> a q e n")
+        for quad in range(4):
+            for a in range(PASSES):
+                nc.sync.dma_start(out=w_plane[32 * quad + 4 * a : 32 * quad + 4 * a + 4].bitcast(I32),
+                                  in_=scale_rows[a, 4 * quad : 4 * quad + 4].bitcast(I32))
         word_rows = w_words.rearrange("e a p n r -> p (e a) (n r)").bitcast(I32)
+        for e0 in range(0, E, 4):
+            nc.sync.dma_start(out=w_codes[:, e0 * PASSES : (e0 + 4) * PASSES, :].bitcast(I32), in_=word_rows[:, e0 * PASSES : (e0 + 4) * PASSES, :])
+        nc.sync.dma_start(first_slots[:], pos1)
+        nc.sync.dma_start(second_slots[:], pos2)
 
-        def load_words(e0, e1):
-            nc.sync.dma_start(out=w_codes[:, e0 * PASSES : e1 * PASSES, :].bitcast(I32), in_=word_rows[:, e0 * PASSES : e1 * PASSES, :])
+        def woven(a, s0, s1):
+            return rounded[a][:, s0:s1, :].rearrange("p (c i) r -> p c r i", i=RUN)
 
-        rounded = {}
+        picked = {}
+        gated = {}
         sums = {}
         done = [0] * len(BANKS)
 
-        last_rounded = y[:, 1536:S].bitcast(BF16).rearrange("p (n r) -> p n r", r=PACK)
-
-        def rounded_slots(a, s0, s1):
-            if a == PASSES - 1 and s0 >= LAST:
-                return last_rounded[:, s0 - LAST : s1 - LAST, :]
-            return rounded[a][:, s0:s1, :]
-
-        def gather(i):
-            a, s0, s1 = STEPS[i]
-            gated = stage.tile([P, PACK, s1 - s0], F32, name="gated", tag="gated_%d" % (i % 2))
+        def pick(a, j):
+            s0, s1 = CUTS[a][j], CUTS[a][j + 1]
+            picked[a, j] = stage.tile([P, PACK, s1 - s0], F32, name="picked", tag="picked", bufs=3)
             for r in range(PACK):
-                cuts = HEAD if (i, r) == (0, 0) else [s0, s1]
-                for c0, c1 in zip(cuts, cuts[1:]):
-                    nc.vector.tensor_tensor(
-                        gated[:, r, c0 - s0 : c1 - s0],
-                        x_rows[a][r][:].indirect(slot_tokens[:, c0 // GROUP : c1 // GROUP]),
-                        gates[:, c0:c1],
-                        MULT,
-                    )
-            if a not in rounded:
-                rounded[a] = stage.tile([P, S, PACK], BF16, name="rounded", tag="rounded_%d" % (a % 2), align_bytes=64)
-            cuts = [s0, s0 + 1024, s1] if s1 - s0 > 1024 else [s0, 1536, LAST, s1]
-            for c0, c1 in zip(cuts, cuts[1:]):
-                nc.scalar.copy(
-                    out=rounded_slots(a, c0, c1).rearrange("p (c i) r -> p c r i", i=4),
-                    in_=gated[:, :, c0 - s0 : c1 - s0].rearrange("p r (c i) -> p c r i", i=4),
-                )
+                nc.scalar.activation(picked[a, j][:, r, :], x_rows[a][r][:].indirect(slot_tokens[:, s0 // GROUP : s1 // GROUP]), COPY)
+
+        def weigh(a, j):
+            s0, s1 = CUTS[a][j], CUTS[a][j + 1]
+            nc.vector.tensor_tensor(
+                woven(a, s0, s1),
+                picked[a, j][:].rearrange("p r (c i) -> p c r i", i=RUN),
+                gates[:, s0:s1].rearrange("p (c o i) -> p c o i", o=1, i=RUN).broadcast_to([P, (s1 - s0) // RUN, PACK, RUN]),
+                MULT,
+            )
+
+        def own_row(a, r):
+            if r == 0:
+                gated[a] = stage.tile([P, PACK, OWN[a]], F32, name="gated", tag="gated")
+            nc.vector.tensor_tensor(gated[a][:, r, :], x_rows[a][r][:].indirect(slot_tokens[:, : OWN[a] // GROUP]), gates[:, : OWN[a]], MULT)
+
+        def own_round(a):
+            nc.vector.tensor_copy(out=woven(a, 0, OWN[a]), in_=gated[a][:].rearrange("p r (c i) -> p c r i", i=RUN))
 
         def quantize(a, s0, s1):
             nc.vector.quantize_mx(
                 out=x_codes[a][:, s0:s1].bitcast(FP8X4),
                 scales=x_plane[:, a, s0:s1],
-                in_=rounded_slots(a, s0, s1).rearrange("p n r -> p (n r)"),
+                in_=rounded[a][:, s0:s1, :].rearrange("p n r -> p (n r)"),
             )
 
         def multiply(a, banks):
@@ -132,51 +137,56 @@ def tile_moe_pre_lin_none_kernel(tc, xT, w_words, w_scales, gate, offs, pos1, po
             e0, e1 = BANKS[b]
             engine_copy(out=y[:, e0 * C : e1 * C], in_=sums[b][:])
 
-        every = range(len(BANKS))
-        gather(0)
-        load_rows(1, range(2))
-        scale_rows = w_scales.rearrange("e a q n -> a q e n")
-        for quad in range(4):
-            for a in range(PASSES):
-                nc.sync.dma_start(out=w_plane[32 * quad + 4 * a : 32 * quad + 4 * a + 4].bitcast(I32),
-                                  in_=scale_rows[a, 4 * quad : 4 * quad + 4].bitcast(I32))
-        for e0 in range(0, E, 4):
-            load_words(e0, e0 + 4)
-        load_rows(1, range(2, PACK))
-        load_rows(2, range(PACK))
-        nc.sync.dma_start(first_slots[:], pos1)
-        nc.sync.dma_start(second_slots[:], pos2)
-        gather(1)
+        pick(0, 0)
+        for r in range(PACK):
+            own_row(0, r)
+        pick(0, 1)
+        weigh(0, 0)
+        own_round(0)
+        own_row(2, 0)
         quantize(0, 0, 1024)
+        multiply(0, [0, 1])
+        own_row(2, 1)
+        pick(1, 0)
+        weigh(0, 1)
+        own_row(2, 2)
         quantize(0, 1024, S)
-        multiply(0, every)
-        gather(2)
-        gather(3)
-        x_codes[1] = stage.tile([P, S], U32, name="x_codes_1", tag="last_row", align_bytes=64)
+        multiply(0, [2, 3, 4, 5])
+        own_row(2, 3)
+        pick(1, 1)
+        weigh(1, 0)
+        own_round(2)
         quantize(1, 0, 1024)
         multiply(1, [0, 1])
+        pick(2, 0)
+        weigh(1, 1)
         quantize(2, 0, 1024)
         multiply(2, [0, 1])
-        quantize(1, 1024, 1536)
-        multiply(1, [2])
+        pick(2, 1)
+        weigh(2, 0)
+        quantize(1, 1024, S)
+        multiply(1, [2, 3, 4, 5])
+        pick(2, 2)
+        weigh(2, 1)
         quantize(2, 1024, 1536)
         multiply(2, [2])
-        quantize(1, 1536, S)
-        multiply(1, [3, 4, 5])
-        quantize(2, 1536, LAST)
+        weigh(2, 2)
+        quantize(2, 1536, 1792)
         multiply(2, [3])
-        quantize(2, LAST, S)
+        quantize(2, 1792, S)
         multiply(2, [4, 5])
-        for b in (0, 1, 2, 5):
+        for b in (0, 1, 2, 3, 4):
             copy_out(nc.scalar.copy, b)
-        for b in (3, 4):
-            copy_out(nc.vector.tensor_copy, b)
+        copy_out(nc.vector.tensor_copy, 5)
 
-        y1 = stage.tile([P, T], F32, name="y1", tag="gated_0")
-        total = stage.tile([P, T], F32, name="total", tag="gated_1")
+        y1 = stage.tile([P, T], F32, name="y1", tag="picked", bufs=3)
+        total = stage.tile([P, T], F32, name="total", tag="gated")
 
-        for t0, t1 in ((0, 640), (640, T)):
-            nc.vector.tensor_copy(y1[:, t0:t1], y[:].indirect(first_slots[:, t0 // GROUP : t1 // GROUP]))
-        for t0, t1 in ((0, 640), (640, 896), (896, T)):
+        back = [0, 160, 480, 800, T]
+        nc.vector.tensor_copy(y1[:, : back[1]], y[:].indirect(first_slots[:, : back[1] // GROUP]))
+        for t0, t1 in zip(back[1:], back[2:]):
+            nc.scalar.activation(y1[:, t0:t1], y[:].indirect(first_slots[:, t0 // GROUP : t1 // GROUP]), COPY)
+        for t0, t1 in zip(back, back[1:]):
             nc.vector.tensor_tensor(total[:, t0:t1], y[:].indirect(second_slots[:, t0 // GROUP : t1 // GROUP]), y1[:, t0:t1], ADD)
+        for t0, t1 in ((0, 480), (480, 800), (800, T)):
             nc.sync.dma_start(out=out[:, t0:t1], in_=total[:, t0:t1])

@@ -1,6 +1,7 @@
 from contextlib import ExitStack
 
 import concourse.mybir as mybir
+from concourse.masks import make_identity
 
 K, T, E, C, N = 1536, 1024, 16, 128, 128
 S = E * C
@@ -26,9 +27,19 @@ GROUP = 16
 PAD = 16
 RUN = 4
 
-OWN = {0: 448, 2: 1024}
-CUTS = [[448, 1024, S], [0, 1024, S], [1024, 1536, 1792, S]]
+BANK = 512
+
+CHUNKS = [
+    (0, 0, 1024, 512, 512),
+    (0, 1024, S, 320, 512),
+    (1, 0, 1024, 320, 512),
+    (1, 1024, S, 320, 512),
+    (2, 0, 1024, 320, 512),
+    (2, 1024, 1536, 128, 160),
+    (2, 1536, S, 0, 160),
+]
 BANKS = [(0, 4), (4, 8), (8, 12), (12, 14), (14, 15), (15, 16)]
+BANK_TAGS = ["bank_0", "bank_1", "bank_2", "bank_3", "gates_0", "gates_1"]
 
 
 def tile_moe_pre_lin_none_kernel(tc, xT, w_words, w_scales, gate, offs, pos1, pos2, out):
@@ -43,14 +54,21 @@ def tile_moe_pre_lin_none_kernel(tc, xT, w_words, w_scales, gate, offs, pos1, po
         second_slots = keep.tile([P, T // GROUP], U16, name="second_slots")
         x_rows = [[keep.tile([P, T + PAD], F32, name="x_row_%d_%d" % (a, r)) for r in range(PACK)] for a in range(PASSES)]
         gates = keep.tile([P, S], F32, name="gates")
+        gate_rows = stage.tile([P, C], F32, name="gate_rows", tag="picked_1")
+        gate_cols = keep.tile([P, E], F32, name="gate_cols")
+        identity = keep.tile([P, P], F32, name="identity")
         w_codes = keep.tile([P, E * PASSES, N], U32, name="w_codes", align_bytes=64)
         w_plane = keep.tile([P, E, N], U8, name="w_plane", align_bytes=64)
-        rounded = [keep.tile([P, S, PACK], BF16, name="rounded_%d" % a, align_bytes=64) for a in range(PASSES)]
         x_codes = [keep.tile([P, S], U32, name="x_codes_%d" % a, align_bytes=64) for a in range(PASSES)]
         x_plane = keep.tile([P, PASSES, S], U8, name="x_plane", align_bytes=64)
         y = keep.tile([P, S], F32, name="y", align_bytes=64)
 
+        idle = keep.tile([P, 2], F32, name="idle")
+        nc.vector.memset(idle[:, 0:1], 0.0)
+        nc.scalar.activation(idle[:, 1:2], idle[:, 0:1], COPY)
+
         nc.vector.memset(w_plane[:].bitcast(I32), 0)
+        make_identity(nc, identity[:])
 
         x_view = xT.rearrange("(a p r) t -> a r p t", p=P, r=PACK)
 
@@ -60,12 +78,12 @@ def tile_moe_pre_lin_none_kernel(tc, xT, w_words, w_scales, gate, offs, pos1, po
 
         load_rows(0, [0])
         nc.sync.dma_start(slot_tokens[:], offs)
-        nc.sync.dma_start(out=gates[:, : OWN[0]], in_=gate[:P, : OWN[0]])
         load_rows(0, range(1, PACK))
-        nc.sync.dma_start(out=gates[:, OWN[0] :], in_=gate[:P, OWN[0] :])
-        load_rows(2, range(2))
+        nc.sync.dma_start(out=gate_rows[:], in_=gate[: P // E, :].rearrange("q (e c) -> (q e) c", c=C))
+        for s0 in (0, 1024):
+            nc.sync.dma_start(out=gates[:, s0 : s0 + 1024], in_=gate[:P, s0 : s0 + 1024])
         load_rows(1, range(PACK))
-        load_rows(2, range(2, PACK))
+        load_rows(2, range(PACK))
         scale_rows = w_scales.rearrange("e a q n -> a q e n")
         for quad in range(4):
             for a in range(PASSES):
@@ -77,49 +95,68 @@ def tile_moe_pre_lin_none_kernel(tc, xT, w_words, w_scales, gate, offs, pos1, po
         nc.sync.dma_start(first_slots[:], pos1)
         nc.sync.dma_start(second_slots[:], pos2)
 
-        def woven(a, s0, s1):
-            return rounded[a][:, s0:s1, :].rearrange("p (c i) r -> p c r i", i=RUN)
+        turned = psum.tile([P, C], F32, name="turned", tag="bank_0")
+        nc.tensor.transpose(turned[:], gate_rows[:], identity[:])
+        nc.vector.tensor_copy(gate_cols[:], turned[:, :E])
+        gate_banks = {}
+        for b in (1, 3, 2, 0):
+            gate_banks[b] = psum.tile([P, BANK], F32, name="gate_bank", tag="gates_%d" % b)
+            for m in range(BANK // C):
+                e = b * (BANK // C) + m
+                nc.tensor.transpose(gate_banks[b][:, m * C : (m + 1) * C], gate_cols[:, e : e + 1].to_broadcast([P, P]), identity[:])
 
         picked = {}
-        gated = {}
+        rounded = {}
         sums = {}
         done = [0] * len(BANKS)
 
-        def pick(a, j):
-            s0, s1 = CUTS[a][j], CUTS[a][j + 1]
-            picked[a, j] = stage.tile([P, PACK, s1 - s0], F32, name="picked", tag="picked", bufs=3)
+        def pick_scalar(j):
+            a, s0, s1, own, pool = CHUNKS[j]
+            picked[j] = stage.tile([P, PACK, s1 - s0], F32, name="picked", tag="picked_%d" % (j % 2 if own else 2))
             for r in range(PACK):
-                nc.scalar.activation(picked[a, j][:, r, :], x_rows[a][r][:].indirect(slot_tokens[:, s0 // GROUP : s1 // GROUP]), COPY)
+                nc.scalar.activation(picked[j][:, r, : s1 - own - s0], x_rows[a][r][:].indirect(slot_tokens[:, s0 // GROUP : (s1 - own) // GROUP]), COPY)
 
-        def weigh(a, j):
-            s0, s1 = CUTS[a][j], CUTS[a][j + 1]
-            nc.vector.tensor_tensor(
-                woven(a, s0, s1),
-                picked[a, j][:].rearrange("p r (c i) -> p c r i", i=RUN),
-                gates[:, s0:s1].rearrange("p (c o i) -> p c o i", o=1, i=RUN).broadcast_to([P, (s1 - s0) // RUN, PACK, RUN]),
+        def pick_vector(j, rows):
+            a, s0, s1, own, pool = CHUNKS[j]
+            for r in rows if own else []:
+                nc.vector.tensor_copy(picked[j][:, r, s1 - own - s0 :], x_rows[a][r][:].indirect(slot_tokens[:, (s1 - own) // GROUP : s1 // GROUP]))
+
+        def weigh(engine, j, c0, c1, factor):
+            s0 = CHUNKS[j][1]
+            engine.tensor_tensor(
+                rounded[j][:, c0 - s0 : c1 - s0, :].rearrange("p (c i) r -> p c r i", i=RUN),
+                picked[j][:, :, c0 - s0 : c1 - s0].rearrange("p r (c i) -> p c r i", i=RUN),
+                factor.rearrange("p (c o i) -> p c o i", o=1, i=RUN).broadcast_to([P, (c1 - c0) // RUN, PACK, RUN]),
                 MULT,
             )
 
-        def own_row(a, r):
-            if r == 0:
-                gated[a] = stage.tile([P, PACK, OWN[a]], F32, name="gated", tag="gated")
-            nc.vector.tensor_tensor(gated[a][:, r, :], x_rows[a][r][:].indirect(slot_tokens[:, : OWN[a] // GROUP]), gates[:, : OWN[a]], MULT)
+        def weigh_chunk(j):
+            a, s0, s1, own, pool = CHUNKS[j]
+            rounded[j] = stage.tile([P, s1 - s0, PACK], BF16, name="rounded", tag="rounded", align_bytes=64)
+            nc.gpsimd.tensor_tensor(
+                rounded[j][:, :pool, :],
+                picked[j][:, :, :pool].rearrange("p r n -> p n r"),
+                gates[:, s0 : s0 + pool].unsqueeze(2).broadcast_to([P, pool, PACK]),
+                MULT,
+            )
+            cuts = [s0 + pool] + [c for c in range(s0 + BANK, s1 + 1, BANK) if c > s0 + pool]
+            for c0, c1 in zip(cuts, cuts[1:]):
+                b = c0 // BANK
+                weigh(nc.vector, j, c0, c1, gate_banks[b][:, c0 - b * BANK : c1 - b * BANK])
 
-        def own_round(a):
-            nc.vector.tensor_copy(out=woven(a, 0, OWN[a]), in_=gated[a][:].rearrange("p r (c i) -> p c r i", i=RUN))
-
-        def quantize(a, s0, s1):
+        def quantize(j, c0, c1):
+            a, s0 = CHUNKS[j][:2]
             nc.vector.quantize_mx(
-                out=x_codes[a][:, s0:s1].bitcast(FP8X4),
-                scales=x_plane[:, a, s0:s1],
-                in_=rounded[a][:, s0:s1, :].rearrange("p n r -> p (n r)"),
+                out=x_codes[a][:, c0:c1].bitcast(FP8X4),
+                scales=x_plane[:, a, c0:c1],
+                in_=rounded[j][:, c0 - s0 : c1 - s0, :].rearrange("p n r -> p (n r)"),
             )
 
         def multiply(a, banks):
             for b in banks:
                 e0, e1 = BANKS[b]
                 if b not in sums:
-                    sums[b] = psum.tile([P, (e1 - e0) * C], F32, name="sums", tag="bank_%d" % b)
+                    sums[b] = psum.tile([P, (e1 - e0) * C], F32, name="sums", tag=BANK_TAGS[b])
                 for e in range(e0, e1):
                     cols = slice(e * C, (e + 1) * C)
                     nc.tensor.matmul_mx(
@@ -137,50 +174,30 @@ def tile_moe_pre_lin_none_kernel(tc, xT, w_words, w_scales, gate, offs, pos1, po
             e0, e1 = BANKS[b]
             engine_copy(out=y[:, e0 * C : e1 * C], in_=sums[b][:])
 
-        pick(0, 0)
-        for r in range(PACK):
-            own_row(0, r)
-        pick(0, 1)
-        weigh(0, 0)
-        own_round(0)
-        own_row(2, 0)
-        quantize(0, 0, 1024)
-        multiply(0, [0, 1])
-        own_row(2, 1)
-        pick(1, 0)
-        weigh(0, 1)
-        own_row(2, 2)
-        quantize(0, 1024, S)
-        multiply(0, [2, 3, 4, 5])
-        own_row(2, 3)
-        pick(1, 1)
-        weigh(1, 0)
-        own_round(2)
-        quantize(1, 0, 1024)
-        multiply(1, [0, 1])
-        pick(2, 0)
-        weigh(1, 1)
-        quantize(2, 0, 1024)
-        multiply(2, [0, 1])
-        pick(2, 1)
-        weigh(2, 0)
-        quantize(1, 1024, S)
-        multiply(1, [2, 3, 4, 5])
-        pick(2, 2)
-        weigh(2, 1)
-        quantize(2, 1024, 1536)
-        multiply(2, [2])
-        weigh(2, 2)
-        quantize(2, 1536, 1792)
+        last = len(CHUNKS) - 1
+        pick_scalar(0)
+        pick_vector(0, range(PACK))
+        for j in range(last):
+            a, s0, s1 = CHUNKS[j][:3]
+            pick_scalar(j + 1)
+            pick_vector(j + 1, range(2))
+            weigh_chunk(j)
+            pick_vector(j + 1, range(2, PACK))
+            quantize(j, s0, s1)
+            multiply(a, [b for b in range(4) if s0 <= BANKS[b][0] * C < s1])
+        multiply(0, [4, 5])
+        multiply(1, [4, 5])
+        weigh_chunk(last)
+        quantize(last, 1536, 1792)
         multiply(2, [3])
-        quantize(2, 1792, S)
+        quantize(last, 1792, S)
         multiply(2, [4, 5])
         for b in (0, 1, 2, 3, 4):
             copy_out(nc.scalar.copy, b)
         copy_out(nc.vector.tensor_copy, 5)
 
-        y1 = stage.tile([P, T], F32, name="y1", tag="picked", bufs=3)
-        total = stage.tile([P, T], F32, name="total", tag="gated")
+        y1 = stage.tile([P, T], F32, name="y1", tag="picked_0")
+        total = stage.tile([P, T], F32, name="total", tag="picked_1")
 
         back = [0, 160, 480, 800, T]
         nc.vector.tensor_copy(y1[:, : back[1]], y[:].indirect(first_slots[:, : back[1] // GROUP]))

@@ -30,13 +30,13 @@ RUN = 4
 BANK = 512
 
 CHUNKS = [
-    (0, 0, 1024, 512, 512),
-    (0, 1024, S, 320, 512),
-    (1, 0, 1024, 320, 512),
-    (1, 1024, S, 320, 512),
-    (2, 0, 1024, 320, 512),
-    (2, 1024, 1536, 128, 160),
-    (2, 1536, S, 0, 160),
+    (0, 0, 1024, [512, 512, 512, 512], 464),
+    (0, 1024, S, [0, 0, 160, 1024], 464),
+    (1, 0, 1024, [0, 0, 160, 1024], 464),
+    (1, 1024, S, [0, 0, 160, 1024], 464),
+    (2, 0, 1024, [0, 0, 160, 1024], 384),
+    (2, 1024, 1536, [0, 0, 0, 512], 128),
+    (2, 1536, S, [0, 0, 0, 0], 128),
 ]
 BANKS = [(0, 4), (4, 8), (8, 12), (12, 14), (14, 15), (15, 16)]
 BANK_TAGS = ["bank_0", "bank_1", "bank_2", "bank_3", "gates_0", "gates_1"]
@@ -98,12 +98,14 @@ def tile_moe_pre_lin_none_kernel(tc, xT, w_words, w_scales, gate, offs, pos1, po
         turned = psum.tile([P, C], F32, name="turned", tag="bank_0")
         nc.tensor.transpose(turned[:], gate_rows[:], identity[:])
         nc.vector.tensor_copy(gate_cols[:], turned[:, :E])
-        gate_banks = {}
-        for b in (1, 3, 2, 0):
-            gate_banks[b] = psum.tile([P, BANK], F32, name="gate_bank", tag="gates_%d" % b)
-            for m in range(BANK // C):
-                e = b * (BANK // C) + m
-                nc.tensor.transpose(gate_banks[b][:, m * C : (m + 1) * C], gate_cols[:, e : e + 1].to_broadcast([P, P]), identity[:])
+        gate_banks = [psum.tile([P, BANK], F32, name="gate_bank", tag="gates_%d" % b) for b in range(S // BANK)]
+        spread = []
+        for a, s0, s1, own, pool in CHUNKS:
+            for e in range((s0 + pool) // C, s1 // C):
+                if e not in spread:
+                    spread.append(e)
+                    b, m = divmod(e, BANK // C)
+                    nc.tensor.transpose(gate_banks[b][:, m * C : (m + 1) * C], gate_cols[:, e : e + 1].to_broadcast([P, P]), identity[:])
 
         picked = {}
         rounded = {}
@@ -112,14 +114,18 @@ def tile_moe_pre_lin_none_kernel(tc, xT, w_words, w_scales, gate, offs, pos1, po
 
         def pick_scalar(j):
             a, s0, s1, own, pool = CHUNKS[j]
-            picked[j] = stage.tile([P, PACK, s1 - s0], F32, name="picked", tag="picked_%d" % (j % 2 if own else 2))
+            picked[j] = stage.tile([P, PACK, s1 - s0], F32, name="picked", tag="picked_%d" % (j % 2))
             for r in range(PACK):
-                nc.scalar.activation(picked[j][:, r, : s1 - own - s0], x_rows[a][r][:].indirect(slot_tokens[:, s0 // GROUP : (s1 - own) // GROUP]), COPY)
+                cut = s1 - own[r]
+                if cut > s0:
+                    nc.scalar.activation(picked[j][:, r, : cut - s0], x_rows[a][r][:].indirect(slot_tokens[:, s0 // GROUP : cut // GROUP]), COPY)
 
         def pick_vector(j, rows):
             a, s0, s1, own, pool = CHUNKS[j]
-            for r in rows if own else []:
-                nc.vector.tensor_copy(picked[j][:, r, s1 - own - s0 :], x_rows[a][r][:].indirect(slot_tokens[:, (s1 - own) // GROUP : s1 // GROUP]))
+            for r in rows:
+                cut = s1 - own[r]
+                if cut < s1:
+                    nc.vector.tensor_copy(picked[j][:, r, cut - s0 :], x_rows[a][r][:].indirect(slot_tokens[:, cut // GROUP : s1 // GROUP]))
 
         def weigh(engine, j, c0, c1, factor):
             s0 = CHUNKS[j][1]
@@ -180,9 +186,10 @@ def tile_moe_pre_lin_none_kernel(tc, xT, w_words, w_scales, gate, offs, pos1, po
         for j in range(last):
             a, s0, s1 = CHUNKS[j][:3]
             pick_scalar(j + 1)
-            pick_vector(j + 1, range(2))
+            ahead = PACK if j == 0 else PACK - 1
+            pick_vector(j + 1, range(ahead))
             weigh_chunk(j)
-            pick_vector(j + 1, range(2, PACK))
+            pick_vector(j + 1, range(ahead, PACK))
             quantize(j, s0, s1)
             multiply(a, [b for b in range(4) if s0 <= BANKS[b][0] * C < s1])
         multiply(0, [4, 5])

@@ -30,14 +30,15 @@ RUN = 4
 BANK = 512
 
 CHUNKS = [
-    (0, 0, 1024, [512, 512, 512, 512], 464),
-    (0, 1024, S, [0, 0, 160, 1024], 464),
-    (1, 0, 1024, [0, 0, 160, 1024], 464),
-    (1, 1024, S, [0, 0, 160, 1024], 464),
+    (0, 0, 1024, [512, 512, 512, 512], 480),
+    (0, 1024, S, [0, 0, 160, 1024], 480),
+    (1, 0, 1024, [0, 0, 160, 1024], 480),
+    (1, 1024, S, [0, 0, 160, 1024], 480),
     (2, 0, 1024, [0, 0, 160, 1024], 384),
     (2, 1024, 1536, [0, 0, 0, 512], 128),
     (2, 1536, S, [0, 0, 0, 0], 128),
 ]
+LAGGED = 4
 BANKS = [(0, 4), (4, 8), (8, 12), (12, 14), (14, 15), (15, 16)]
 BANK_TAGS = ["bank_0", "bank_1", "bank_2", "bank_3", "gates_0", "gates_1"]
 
@@ -138,7 +139,7 @@ def tile_moe_pre_lin_none_kernel(tc, xT, w_words, w_scales, gate, offs, pos1, po
 
         def weigh_chunk(j):
             a, s0, s1, own, pool = CHUNKS[j]
-            rounded[j] = stage.tile([P, s1 - s0, PACK], BF16, name="rounded", tag="rounded", align_bytes=64)
+            rounded[j] = stage.tile([P, s1 - s0, PACK], BF16, name="rounded", tag="rounded_%d" % (min(j, LAGGED) % 3), align_bytes=64)
             nc.gpsimd.tensor_tensor(
                 rounded[j][:, :pool, :],
                 picked[j][:, :, :pool].rearrange("p r n -> p n r"),
@@ -190,8 +191,10 @@ def tile_moe_pre_lin_none_kernel(tc, xT, w_words, w_scales, gate, offs, pos1, po
             pick_vector(j + 1, range(ahead))
             weigh_chunk(j)
             pick_vector(j + 1, range(ahead, PACK))
-            quantize(j, s0, s1)
-            multiply(a, [b for b in range(4) if s0 <= BANKS[b][0] * C < s1])
+            for i in ([j - 1] if 0 < j <= LAGGED else []) + ([j] if j >= LAGGED else []):
+                a, s0, s1 = CHUNKS[i][:3]
+                quantize(i, s0, s1)
+                multiply(a, [b for b in range(4) if s0 <= BANKS[b][0] * C < s1])
         multiply(0, [4, 5])
         multiply(1, [4, 5])
         weigh_chunk(last)
@@ -206,11 +209,11 @@ def tile_moe_pre_lin_none_kernel(tc, xT, w_words, w_scales, gate, offs, pos1, po
         y1 = stage.tile([P, T], F32, name="y1", tag="picked_0")
         total = stage.tile([P, T], F32, name="total", tag="picked_1")
 
-        back = [0, 160, 480, 800, T]
+        back = [0, 192, 576, 896, T]
         nc.vector.tensor_copy(y1[:, : back[1]], y[:].indirect(first_slots[:, : back[1] // GROUP]))
         for t0, t1 in zip(back[1:], back[2:]):
             nc.scalar.activation(y1[:, t0:t1], y[:].indirect(first_slots[:, t0 // GROUP : t1 // GROUP]), COPY)
         for t0, t1 in zip(back, back[1:]):
             nc.vector.tensor_tensor(total[:, t0:t1], y[:].indirect(second_slots[:, t0 // GROUP : t1 // GROUP]), y1[:, t0:t1], ADD)
-        for t0, t1 in ((0, 480), (480, 800), (800, T)):
+        for t0, t1 in ((0, 576), (576, 896), (896, T)):
             nc.sync.dma_start(out=out[:, t0:t1], in_=total[:, t0:t1])

@@ -30,15 +30,16 @@ RUN = 4
 BANK = 512
 
 CHUNKS = [
-    (0, 0, 1024, [512, 512, 512, 512], 480),
-    (0, 1024, S, [0, 0, 160, 1024], 480),
-    (1, 0, 1024, [0, 0, 160, 1024], 480),
-    (1, 1024, S, [0, 0, 160, 1024], 480),
-    (2, 0, 1024, [0, 0, 160, 1024], 384),
-    (2, 1024, 1536, [0, 0, 0, 512], 128),
-    (2, 1536, S, [0, 0, 0, 0], 128),
+    (0, 0, 1024, [512, 512, 512, 512], 448),
+    (0, 1024, S, [0, 0, 192, 1024], 448),
+    (1, 0, 1024, [0, 0, 192, 1024], 448),
+    (1, 1024, S, [0, 0, 192, 1024], 448),
+    (2, 0, 1024, [0, 0, 192, 1024], 368),
+    (2, 1024, 1792, [0, 0, 0, 512], 208),
+    (2, 1792, S, [0, 0, 0, 0], 0),
 ]
 LAGGED = 4
+ROUNDED_TAGS = ["rounded_0", "rounded_1", "rounded_2", "rounded_0", "rounded_1", "rounded_1", "rounded_2"]
 BANKS = [(0, 4), (4, 8), (8, 12), (12, 14), (14, 15), (15, 16)]
 BANK_TAGS = ["bank_0", "bank_1", "bank_2", "bank_3", "gates_0", "gates_1"]
 
@@ -55,7 +56,7 @@ def tile_moe_pre_lin_none_kernel(tc, xT, w_words, w_scales, gate, offs, pos1, po
         second_slots = keep.tile([P, T // GROUP], U16, name="second_slots")
         x_rows = [[keep.tile([P, T + PAD], F32, name="x_row_%d_%d" % (a, r)) for r in range(PACK)] for a in range(PASSES)]
         gates = keep.tile([P, S], F32, name="gates")
-        gate_rows = stage.tile([P, C], F32, name="gate_rows", tag="picked_1")
+        gate_rows = stage.tile([P, C], F32, name="gate_rows", tag="picked_1", align_bytes=64)
         gate_cols = keep.tile([P, E], F32, name="gate_cols")
         identity = keep.tile([P, P], F32, name="identity")
         w_codes = keep.tile([P, E * PASSES, N], U32, name="w_codes", align_bytes=64)
@@ -115,7 +116,7 @@ def tile_moe_pre_lin_none_kernel(tc, xT, w_words, w_scales, gate, offs, pos1, po
 
         def pick_scalar(j):
             a, s0, s1, own, pool = CHUNKS[j]
-            picked[j] = stage.tile([P, PACK, s1 - s0], F32, name="picked", tag="picked_%d" % (j % 2))
+            picked[j] = stage.tile([P, PACK, s1 - s0], F32, name="picked", tag="picked_%d" % (j % 2), align_bytes=64)
             for r in range(PACK):
                 cut = s1 - own[r]
                 if cut > s0:
@@ -139,14 +140,15 @@ def tile_moe_pre_lin_none_kernel(tc, xT, w_words, w_scales, gate, offs, pos1, po
 
         def weigh_chunk(j):
             a, s0, s1, own, pool = CHUNKS[j]
-            rounded[j] = stage.tile([P, s1 - s0, PACK], BF16, name="rounded", tag="rounded_%d" % (min(j, LAGGED) % 3), align_bytes=64)
-            nc.gpsimd.tensor_tensor(
-                rounded[j][:, :pool, :],
-                picked[j][:, :, :pool].rearrange("p r n -> p n r"),
-                gates[:, s0 : s0 + pool].unsqueeze(2).broadcast_to([P, pool, PACK]),
-                MULT,
-            )
-            cuts = [s0 + pool] + [c for c in range(s0 + BANK, s1 + 1, BANK) if c > s0 + pool]
+            rounded[j] = stage.tile([P, s1 - s0, PACK], BF16, name="rounded", tag=ROUNDED_TAGS[j], align_bytes=64)
+            if pool:
+                nc.gpsimd.tensor_tensor(
+                    rounded[j][:, :pool, :],
+                    picked[j][:, :, :pool].rearrange("p r n -> p n r"),
+                    gates[:, s0 : s0 + pool].unsqueeze(2).broadcast_to([P, pool, PACK]),
+                    MULT,
+                )
+            cuts = [s0 + pool] + [c for c in range(BANK, s1, BANK) if c > s0 + pool] + [s1]
             for c0, c1 in zip(cuts, cuts[1:]):
                 b = c0 // BANK
                 weigh(nc.vector, j, c0, c1, gate_banks[b][:, c0 - b * BANK : c1 - b * BANK])
@@ -181,7 +183,7 @@ def tile_moe_pre_lin_none_kernel(tc, xT, w_words, w_scales, gate, offs, pos1, po
             e0, e1 = BANKS[b]
             engine_copy(out=y[:, e0 * C : e1 * C], in_=sums[b][:])
 
-        last = len(CHUNKS) - 1
+        last = LAGGED + 1
         pick_scalar(0)
         pick_vector(0, range(PACK))
         for j in range(last):
@@ -197,17 +199,21 @@ def tile_moe_pre_lin_none_kernel(tc, xT, w_words, w_scales, gate, offs, pos1, po
                 multiply(a, [b for b in range(4) if s0 <= BANKS[b][0] * C < s1])
         multiply(0, [4, 5])
         multiply(1, [4, 5])
+        pick_scalar(last + 1)
         weigh_chunk(last)
+        quantize(last, 1024, 1536)
+        multiply(2, [2])
+        weigh_chunk(last + 1)
         quantize(last, 1536, 1792)
         multiply(2, [3])
-        quantize(last, 1792, S)
+        quantize(last + 1, 1792, S)
         multiply(2, [4, 5])
         for b in (0, 1, 2, 3, 4):
             copy_out(nc.scalar.copy, b)
         copy_out(nc.vector.tensor_copy, 5)
 
-        y1 = stage.tile([P, T], F32, name="y1", tag="picked_0")
-        total = stage.tile([P, T], F32, name="total", tag="picked_1")
+        y1 = stage.tile([P, T], F32, name="y1", tag="picked_0", align_bytes=64)
+        total = stage.tile([P, T], F32, name="total", tag="picked_1", align_bytes=64)
 
         back = [0, 192, 576, 896, T]
         nc.vector.tensor_copy(y1[:, : back[1]], y[:].indirect(first_slots[:, : back[1] // GROUP]))

@@ -26,22 +26,29 @@ PASSES = K // (P * PACK)
 GROUP = 16
 PAD = 16
 RUN = 4
-
 BANK = 512
+WIDE = 1024
+TAIL = 2 * C
 
+THIRD_ROW = 192
+POOL_FULL = 448
+POOL_LATE, POOL_LAST = 336, 192
+LATE_ROW = 512
+
+STEADY = [0, 0, THIRD_ROW, WIDE]
 CHUNKS = [
-    (0, 0, 1024, [512, 512, 512, 512], 448),
-    (0, 1024, S, [0, 0, 192, 1024], 448),
-    (1, 0, 1024, [0, 0, 192, 1024], 448),
-    (1, 1024, S, [0, 0, 192, 1024], 448),
-    (2, 0, 1024, [0, 0, 192, 1024], 368),
-    (2, 1024, 1792, [0, 0, 0, 512], 208),
-    (2, 1792, S, [0, 0, 0, 0], 0),
+    (0, 0, WIDE, [WIDE // 2] * PACK, POOL_FULL),
+    (0, WIDE, S, STEADY, POOL_FULL),
+    (1, 0, WIDE, STEADY, POOL_FULL),
+    (1, WIDE, S, STEADY, POOL_FULL),
+    (2, 0, WIDE, STEADY, POOL_LATE),
+    (2, WIDE, S - TAIL, [0, 0, 0, LATE_ROW], POOL_LAST),
+    (2, S - TAIL, S, [0] * PACK, 0),
 ]
-LAGGED = 4
-ROUNDED_TAGS = ["rounded_0", "rounded_1", "rounded_2", "rounded_0", "rounded_1", "rounded_1", "rounded_2"]
 BANKS = [(0, 4), (4, 8), (8, 12), (12, 14), (14, 15), (15, 16)]
-BANK_TAGS = ["bank_0", "bank_1", "bank_2", "bank_3", "gates_0", "gates_1"]
+BANK_TAGS = ["sums_0", "sums_1", "sums_2", "sums_3", "gates_0", "gates_1"]
+EARLY_BANKS, LATE_BANKS = range(4), (4, 5)
+BACK = [0, 192, 576, 896, T]
 
 
 def tile_moe_pre_lin_none_kernel(tc, xT, w_words, w_scales, gate, offs, pos1, pos2, out):
@@ -55,8 +62,8 @@ def tile_moe_pre_lin_none_kernel(tc, xT, w_words, w_scales, gate, offs, pos1, po
         first_slots = keep.tile([P, T // GROUP], U16, name="first_slots")
         second_slots = keep.tile([P, T // GROUP], U16, name="second_slots")
         x_rows = [[keep.tile([P, T + PAD], F32, name="x_row_%d_%d" % (a, r)) for r in range(PACK)] for a in range(PASSES)]
-        gates = keep.tile([P, S], F32, name="gates")
-        gate_rows = stage.tile([P, C], F32, name="gate_rows", tag="picked_1", align_bytes=64)
+        pool_gates = {s0: keep.tile([P, POOL_FULL], F32, name="pool_gates_%d" % s0) for s0 in (0, WIDE)}
+        gate_rows = stage.tile([P, C], F32, name="gate_rows", tag="picked_1")
         gate_cols = keep.tile([P, E], F32, name="gate_cols")
         identity = keep.tile([P, P], F32, name="identity")
         w_codes = keep.tile([P, E * PASSES, N], U32, name="w_codes", align_bytes=64)
@@ -82,8 +89,8 @@ def tile_moe_pre_lin_none_kernel(tc, xT, w_words, w_scales, gate, offs, pos1, po
         nc.sync.dma_start(slot_tokens[:], offs)
         load_rows(0, range(1, PACK))
         nc.sync.dma_start(out=gate_rows[:], in_=gate[: P // E, :].rearrange("q (e c) -> (q e) c", c=C))
-        for s0 in (0, 1024):
-            nc.sync.dma_start(out=gates[:, s0 : s0 + 1024], in_=gate[:P, s0 : s0 + 1024])
+        for s0 in (0, WIDE):
+            nc.sync.dma_start(out=pool_gates[s0][:], in_=gate[:P, s0 : s0 + POOL_FULL])
         load_rows(1, range(PACK))
         load_rows(2, range(PACK))
         scale_rows = w_scales.rearrange("e a q n -> a q e n")
@@ -93,11 +100,12 @@ def tile_moe_pre_lin_none_kernel(tc, xT, w_words, w_scales, gate, offs, pos1, po
                                   in_=scale_rows[a, 4 * quad : 4 * quad + 4].bitcast(I32))
         word_rows = w_words.rearrange("e a p n r -> p (e a) (n r)").bitcast(I32)
         for e0 in range(0, E, 4):
-            nc.sync.dma_start(out=w_codes[:, e0 * PASSES : (e0 + 4) * PASSES, :].bitcast(I32), in_=word_rows[:, e0 * PASSES : (e0 + 4) * PASSES, :])
+            rows = slice(e0 * PASSES, (e0 + 4) * PASSES)
+            nc.sync.dma_start(out=w_codes[:, rows, :].bitcast(I32), in_=word_rows[:, rows, :])
         nc.sync.dma_start(first_slots[:], pos1)
         nc.sync.dma_start(second_slots[:], pos2)
 
-        turned = psum.tile([P, C], F32, name="turned", tag="bank_0")
+        turned = psum.tile([P, C], F32, name="turned", tag="sums_0")
         nc.tensor.transpose(turned[:], gate_rows[:], identity[:])
         nc.vector.tensor_copy(gate_cols[:], turned[:, :E])
         gate_banks = [psum.tile([P, BANK], F32, name="gate_bank", tag="gates_%d" % b) for b in range(S // BANK)]
@@ -112,46 +120,43 @@ def tile_moe_pre_lin_none_kernel(tc, xT, w_words, w_scales, gate, offs, pos1, po
         picked = {}
         rounded = {}
         sums = {}
-        done = [0] * len(BANKS)
+        issued = [0] * len(BANKS)
 
-        def pick_scalar(j):
+        def gather_on_scalar(j):
             a, s0, s1, own, pool = CHUNKS[j]
-            picked[j] = stage.tile([P, PACK, s1 - s0], F32, name="picked", tag="picked_%d" % (j % 2), align_bytes=64)
+            picked[j] = stage.tile([P, PACK, s1 - s0], F32, name="picked", tag="picked_%d" % (j % 2))
             for r in range(PACK):
                 cut = s1 - own[r]
                 if cut > s0:
                     nc.scalar.activation(picked[j][:, r, : cut - s0], x_rows[a][r][:].indirect(slot_tokens[:, s0 // GROUP : cut // GROUP]), COPY)
 
-        def pick_vector(j, rows):
+        def gather_on_vector(j, rows):
             a, s0, s1, own, pool = CHUNKS[j]
             for r in rows:
                 cut = s1 - own[r]
                 if cut < s1:
                     nc.vector.tensor_copy(picked[j][:, r, cut - s0 :], x_rows[a][r][:].indirect(slot_tokens[:, cut // GROUP : s1 // GROUP]))
 
-        def weigh(engine, j, c0, c1, factor):
-            s0 = CHUNKS[j][1]
-            engine.tensor_tensor(
-                rounded[j][:, c0 - s0 : c1 - s0, :].rearrange("p (c i) r -> p c r i", i=RUN),
-                picked[j][:, :, c0 - s0 : c1 - s0].rearrange("p r (c i) -> p c r i", i=RUN),
-                factor.rearrange("p (c o i) -> p c o i", o=1, i=RUN).broadcast_to([P, (c1 - c0) // RUN, PACK, RUN]),
-                MULT,
-            )
-
-        def weigh_chunk(j):
+        def weigh(j):
             a, s0, s1, own, pool = CHUNKS[j]
-            rounded[j] = stage.tile([P, s1 - s0, PACK], BF16, name="rounded", tag=ROUNDED_TAGS[j], align_bytes=64)
+            rounded[j] = stage.tile([P, s1 - s0, PACK], BF16, name="rounded", tag="rounded_shared" if pool else "rounded_tail", align_bytes=64)
             if pool:
                 nc.gpsimd.tensor_tensor(
                     rounded[j][:, :pool, :],
                     picked[j][:, :, :pool].rearrange("p r n -> p n r"),
-                    gates[:, s0 : s0 + pool].unsqueeze(2).broadcast_to([P, pool, PACK]),
+                    pool_gates[s0][:, :pool].unsqueeze(2).broadcast_to([P, pool, PACK]),
                     MULT,
                 )
             cuts = [s0 + pool] + [c for c in range(BANK, s1, BANK) if c > s0 + pool] + [s1]
             for c0, c1 in zip(cuts, cuts[1:]):
                 b = c0 // BANK
-                weigh(nc.vector, j, c0, c1, gate_banks[b][:, c0 - b * BANK : c1 - b * BANK])
+                factor = gate_banks[b][:, c0 - b * BANK : c1 - b * BANK].rearrange("p (c o i) -> p c o i", o=1, i=RUN)
+                nc.vector.tensor_tensor(
+                    rounded[j][:, c0 - s0 : c1 - s0, :].rearrange("p (c i) r -> p c r i", i=RUN),
+                    picked[j][:, :, c0 - s0 : c1 - s0].rearrange("p r (c i) -> p c r i", i=RUN),
+                    factor.broadcast_to([P, (c1 - c0) // RUN, PACK, RUN]),
+                    MULT,
+                )
 
         def quantize(j, c0, c1):
             a, s0 = CHUNKS[j][:2]
@@ -174,52 +179,50 @@ def tile_moe_pre_lin_none_kernel(tc, xT, w_words, w_scales, gate, offs, pos1, po
                         lhsT_scale=w_plane[4 * a :, e, :],
                         rhs=x_codes[a][:, cols].bitcast(FP8X4),
                         rhs_scale=x_plane[:, a, cols],
-                        start=(done[b] == 0),
-                        stop=(done[b] == PASSES * (e1 - e0) - 1),
+                        start=(issued[b] == 0),
+                        stop=(issued[b] == PASSES * (e1 - e0) - 1),
                     )
-                    done[b] += 1
+                    issued[b] += 1
 
         def copy_out(engine_copy, b):
             e0, e1 = BANKS[b]
             engine_copy(out=y[:, e0 * C : e1 * C], in_=sums[b][:])
 
-        last = LAGGED + 1
-        pick_scalar(0)
-        pick_vector(0, range(PACK))
-        for j in range(last):
+        last = len(CHUNKS) - 1
+        gather_on_scalar(0)
+        gather_on_vector(0, range(PACK))
+        for j in range(last - 1):
             a, s0, s1 = CHUNKS[j][:3]
-            pick_scalar(j + 1)
+            gather_on_scalar(j + 1)
             ahead = PACK if j == 0 else PACK - 1
-            pick_vector(j + 1, range(ahead))
-            weigh_chunk(j)
-            pick_vector(j + 1, range(ahead, PACK))
-            for i in ([j - 1] if 0 < j <= LAGGED else []) + ([j] if j >= LAGGED else []):
-                a, s0, s1 = CHUNKS[i][:3]
-                quantize(i, s0, s1)
-                multiply(a, [b for b in range(4) if s0 <= BANKS[b][0] * C < s1])
-        multiply(0, [4, 5])
-        multiply(1, [4, 5])
-        pick_scalar(last + 1)
-        weigh_chunk(last)
-        quantize(last, 1024, 1536)
-        multiply(2, [2])
-        weigh_chunk(last + 1)
-        quantize(last, 1536, 1792)
-        multiply(2, [3])
-        quantize(last + 1, 1792, S)
-        multiply(2, [4, 5])
-        for b in (0, 1, 2, 3, 4):
+            gather_on_vector(j + 1, range(ahead))
+            weigh(j)
+            gather_on_vector(j + 1, range(ahead, PACK))
+            quantize(j, s0, s1)
+            multiply(a, [b for b in EARLY_BANKS if s0 <= BANKS[b][0] * C < s1])
+        for a in range(PASSES - 1):
+            multiply(a, LATE_BANKS)
+
+        gather_on_scalar(last)
+        weigh(last - 1)
+        quantize(last - 1, WIDE, WIDE + BANK)
+        multiply(PASSES - 1, [2])
+        weigh(last)
+        quantize(last - 1, WIDE + BANK, S - TAIL)
+        multiply(PASSES - 1, [3])
+        quantize(last, S - TAIL, S)
+        multiply(PASSES - 1, LATE_BANKS)
+        for b in range(len(BANKS) - 1):
             copy_out(nc.scalar.copy, b)
-        copy_out(nc.vector.tensor_copy, 5)
+        copy_out(nc.vector.tensor_copy, len(BANKS) - 1)
 
-        y1 = stage.tile([P, T], F32, name="y1", tag="picked_0", align_bytes=64)
-        total = stage.tile([P, T], F32, name="total", tag="picked_1", align_bytes=64)
-
-        back = [0, 192, 576, 896, T]
-        nc.vector.tensor_copy(y1[:, : back[1]], y[:].indirect(first_slots[:, : back[1] // GROUP]))
-        for t0, t1 in zip(back[1:], back[2:]):
-            nc.scalar.activation(y1[:, t0:t1], y[:].indirect(first_slots[:, t0 // GROUP : t1 // GROUP]), COPY)
-        for t0, t1 in zip(back, back[1:]):
-            nc.vector.tensor_tensor(total[:, t0:t1], y[:].indirect(second_slots[:, t0 // GROUP : t1 // GROUP]), y1[:, t0:t1], ADD)
-        for t0, t1 in ((0, 576), (576, 896), (896, T)):
+        first_results = stage.tile([P, T], F32, name="first_results", tag="picked_0")
+        total = stage.tile([P, T], F32, name="total", tag="picked_1")
+        pieces = list(zip(BACK, BACK[1:]))
+        nc.vector.tensor_copy(first_results[:, : BACK[1]], y[:].indirect(first_slots[:, : BACK[1] // GROUP]))
+        for t0, t1 in pieces[1:]:
+            nc.scalar.activation(first_results[:, t0:t1], y[:].indirect(first_slots[:, t0 // GROUP : t1 // GROUP]), COPY)
+        for t0, t1 in pieces:
+            nc.vector.tensor_tensor(total[:, t0:t1], y[:].indirect(second_slots[:, t0 // GROUP : t1 // GROUP]), first_results[:, t0:t1], ADD)
+        for t0, t1 in [(0, BACK[2])] + pieces[2:]:
             nc.sync.dma_start(out=out[:, t0:t1], in_=total[:, t0:t1])

@@ -26,13 +26,14 @@ PASSES = K // (P * PACK)
 GROUP = 16
 PAD = 16
 RUN = 4
+PAIR = 2
 BANK = 512
 WIDE = 1024
 TAIL = 2 * C
 
-THIRD_ROW = 192
-POOL_FULL = 448
-POOL_LATE, POOL_LAST = 336, 192
+THIRD_ROW = 288
+POOL_FULL = 544
+POOL_LATE, POOL_LAST = 400, 224
 LATE_ROW = 512
 
 STEADY = [0, 0, THIRD_ROW, WIDE]
@@ -142,9 +143,9 @@ def tile_moe_pre_lin_none_kernel(tc, xT, w_words, w_scales, gate, offs, pos1, po
             rounded[j] = stage.tile([P, s1 - s0, PACK], BF16, name="rounded", tag="rounded_shared" if pool else "rounded_tail", align_bytes=64)
             if pool:
                 nc.gpsimd.tensor_tensor(
-                    rounded[j][:, :pool, :],
-                    picked[j][:, :, :pool].rearrange("p r n -> p n r"),
-                    pool_gates[s0][:, :pool].unsqueeze(2).broadcast_to([P, pool, PACK]),
+                    rounded[j][:, :pool, :].rearrange("p (c i) r -> p c r i", i=PAIR),
+                    picked[j][:, :, :pool].rearrange("p r (c i) -> p c r i", i=PAIR),
+                    pool_gates[s0][:, :pool].rearrange("p (c o i) -> p c o i", o=1, i=PAIR).broadcast_to([P, pool // PAIR, PACK, PAIR]),
                     MULT,
                 )
             cuts = [s0 + pool] + [c for c in range(BANK, s1, BANK) if c > s0 + pool] + [s1]

@@ -31,7 +31,7 @@ BANK = 512
 WIDE = 1024
 TAIL = 2 * C
 
-THIRD_ROW = 288
+THIRD_ROW = 320
 POOL_FULL = 544
 POOL_LATE, POOL_LAST = 400, 224
 LATE_ROW = 512

@@ -26,15 +26,14 @@ PASSES = K // (P * PACK)
 GROUP = 16
 PAD = 16
 RUN = 4
-PAIR = 2
 BANK = 512
 WIDE = 1024
 TAIL = 2 * C
 
 THIRD_ROW = 320
 POOL_FULL = 544
-POOL_LATE, POOL_LAST = 400, 224
-LATE_ROW = 512
+POOL_LATE, POOL_LAST = 424, 224
+LATE_ROW = 640
 
 STEADY = [0, 0, THIRD_ROW, WIDE]
 CHUNKS = [
@@ -143,9 +142,9 @@ def tile_moe_pre_lin_none_kernel(tc, xT, w_words, w_scales, gate, offs, pos1, po
             rounded[j] = stage.tile([P, s1 - s0, PACK], BF16, name="rounded", tag="rounded_shared" if pool else "rounded_tail", align_bytes=64)
             if pool:
                 nc.gpsimd.tensor_tensor(
-                    rounded[j][:, :pool, :].rearrange("p (c i) r -> p c r i", i=PAIR),
-                    picked[j][:, :, :pool].rearrange("p r (c i) -> p c r i", i=PAIR),
-                    pool_gates[s0][:, :pool].rearrange("p (c o i) -> p c o i", o=1, i=PAIR).broadcast_to([P, pool // PAIR, PACK, PAIR]),
+                    rounded[j][:, :pool, :].rearrange("p (c i) r -> p c r i", i=RUN),
+                    picked[j][:, :, :pool].rearrange("p r (c i) -> p c r i", i=RUN),
+                    pool_gates[s0][:, :pool].rearrange("p (c o i) -> p c o i", o=1, i=RUN).broadcast_to([P, pool // RUN, PACK, RUN]),
                     MULT,
                 )
             cuts = [s0 + pool] + [c for c in range(BANK, s1, BANK) if c > s0 + pool] + [s1]

@@ -30,9 +30,9 @@ BANK = 512
 WIDE = 1024
 TAIL = 2 * C
 
-THIRD_ROW = 320
-POOL_FULL = 544
-POOL_LATE, POOL_LAST = 424, 224
+THIRD_ROW = 352
+POOL_FULL = 576
+POOL_LATE, POOL_LAST = 448, 224
 LATE_ROW = 640
 
 STEADY = [0, 0, THIRD_ROW, WIDE]
@@ -45,10 +45,17 @@ CHUNKS = [
     (2, WIDE, S - TAIL, [0, 0, 0, LATE_ROW], POOL_LAST),
     (2, S - TAIL, S, [0] * PACK, 0),
 ]
+CALLS = [0, 256, 640, WIDE]
+LATE_CALLS = [0, 512, WIDE]
 BANKS = [(0, 4), (4, 8), (8, 12), (12, 14), (14, 15), (15, 16)]
 BANK_TAGS = ["sums_0", "sums_1", "sums_2", "sums_3", "gates_0", "gates_1"]
 EARLY_BANKS, LATE_BANKS = range(4), (4, 5)
 BACK = [0, 192, 576, 896, T]
+
+
+def shares(j):
+    a, s0, s1, own, pool = CHUNKS[j]
+    return ((s0 + pool, s1), (s0, s0 + pool)) if s0 else ((s0, s1 - pool), (s1 - pool, s1))
 
 
 def tile_moe_pre_lin_none_kernel(tc, xT, w_words, w_scales, gate, offs, pos1, pos2, out):
@@ -62,7 +69,7 @@ def tile_moe_pre_lin_none_kernel(tc, xT, w_words, w_scales, gate, offs, pos1, po
         first_slots = keep.tile([P, T // GROUP], U16, name="first_slots")
         second_slots = keep.tile([P, T // GROUP], U16, name="second_slots")
         x_rows = [[keep.tile([P, T + PAD], F32, name="x_row_%d_%d" % (a, r)) for r in range(PACK)] for a in range(PASSES)]
-        pool_gates = {s0: keep.tile([P, POOL_FULL], F32, name="pool_gates_%d" % s0) for s0 in (0, WIDE)}
+        pool_gates = {g0: keep.tile([P, POOL_FULL], F32, name="pool_gates_%d" % g0) for g0 in (WIDE - POOL_FULL, WIDE)}
         gate_rows = stage.tile([P, C], F32, name="gate_rows", tag="picked_1")
         gate_cols = keep.tile([P, E], F32, name="gate_cols")
         identity = keep.tile([P, P], F32, name="identity")
@@ -71,6 +78,8 @@ def tile_moe_pre_lin_none_kernel(tc, xT, w_words, w_scales, gate, offs, pos1, po
         x_codes = [keep.tile([P, S], U32, name="x_codes_%d" % a, align_bytes=64) for a in range(PASSES)]
         x_plane = keep.tile([P, PASSES, S], U8, name="x_plane", align_bytes=64)
         y = keep.tile([P, S], F32, name="y", align_bytes=64)
+        rounded_shared = keep.tile([P, WIDE, PACK], BF16, name="rounded_shared", align_bytes=64)
+        rounded_tail = keep.tile([P, TAIL, PACK], BF16, name="rounded_tail", align_bytes=64)
 
         idle = keep.tile([P, 2], F32, name="idle")
         nc.vector.memset(idle[:, 0:1], 0.0)
@@ -89,8 +98,8 @@ def tile_moe_pre_lin_none_kernel(tc, xT, w_words, w_scales, gate, offs, pos1, po
         nc.sync.dma_start(slot_tokens[:], offs)
         load_rows(0, range(1, PACK))
         nc.sync.dma_start(out=gate_rows[:], in_=gate[: P // E, :].rearrange("q (e c) -> (q e) c", c=C))
-        for s0 in (0, WIDE):
-            nc.sync.dma_start(out=pool_gates[s0][:], in_=gate[:P, s0 : s0 + POOL_FULL])
+        for g0 in pool_gates:
+            nc.sync.dma_start(out=pool_gates[g0][:], in_=gate[:P, g0 : g0 + POOL_FULL])
         load_rows(1, range(PACK))
         load_rows(2, range(PACK))
         scale_rows = w_scales.rearrange("e a q n -> a q e n")
@@ -110,15 +119,15 @@ def tile_moe_pre_lin_none_kernel(tc, xT, w_words, w_scales, gate, offs, pos1, po
         nc.vector.tensor_copy(gate_cols[:], turned[:, :E])
         gate_banks = [psum.tile([P, BANK], F32, name="gate_bank", tag="gates_%d" % b) for b in range(S // BANK)]
         spread = []
-        for a, s0, s1, own, pool in CHUNKS:
-            for e in range((s0 + pool) // C, s1 // C):
+        for j in range(len(CHUNKS)):
+            v0, v1 = shares(j)[0]
+            for e in range(v0 // C, -(-v1 // C)):
                 if e not in spread:
                     spread.append(e)
                     b, m = divmod(e, BANK // C)
                     nc.tensor.transpose(gate_banks[b][:, m * C : (m + 1) * C], gate_cols[:, e : e + 1].to_broadcast([P, P]), identity[:])
 
         picked = {}
-        rounded = {}
         sums = {}
         issued = [0] * len(BANKS)
 
@@ -137,33 +146,38 @@ def tile_moe_pre_lin_none_kernel(tc, xT, w_words, w_scales, gate, offs, pos1, po
                 if cut < s1:
                     nc.vector.tensor_copy(picked[j][:, r, cut - s0 :], x_rows[a][r][:].indirect(slot_tokens[:, cut // GROUP : s1 // GROUP]))
 
+        def rounded(j, c0, c1):
+            s0, pool = CHUNKS[j][1], CHUNKS[j][4]
+            return (rounded_shared if pool else rounded_tail)[:, c0 - s0 : c1 - s0, :]
+
         def weigh(j):
-            a, s0, s1, own, pool = CHUNKS[j]
-            rounded[j] = stage.tile([P, s1 - s0, PACK], BF16, name="rounded", tag="rounded_shared" if pool else "rounded_tail", align_bytes=64)
-            if pool:
+            s0 = CHUNKS[j][1]
+            (v0, v1), (p0, p1) = shares(j)
+            if p1 > p0:
+                g0 = WIDE if s0 else WIDE - POOL_FULL
                 nc.gpsimd.tensor_tensor(
-                    rounded[j][:, :pool, :].rearrange("p (c i) r -> p c r i", i=RUN),
-                    picked[j][:, :, :pool].rearrange("p r (c i) -> p c r i", i=RUN),
-                    pool_gates[s0][:, :pool].rearrange("p (c o i) -> p c o i", o=1, i=RUN).broadcast_to([P, pool // RUN, PACK, RUN]),
+                    rounded(j, p0, p1).rearrange("p (c i) r -> p c r i", i=RUN),
+                    picked[j][:, :, p0 - s0 : p1 - s0].rearrange("p r (c i) -> p c r i", i=RUN),
+                    pool_gates[g0][:, p0 - g0 : p1 - g0].rearrange("p (c o i) -> p c o i", o=1, i=RUN).broadcast_to([P, (p1 - p0) // RUN, PACK, RUN]),
                     MULT,
                 )
-            cuts = [s0 + pool] + [c for c in range(BANK, s1, BANK) if c > s0 + pool] + [s1]
+            cuts = [v0] + [c for c in range(BANK, v1, BANK) if c > v0] + [v1]
             for c0, c1 in zip(cuts, cuts[1:]):
                 b = c0 // BANK
                 factor = gate_banks[b][:, c0 - b * BANK : c1 - b * BANK].rearrange("p (c o i) -> p c o i", o=1, i=RUN)
                 nc.vector.tensor_tensor(
-                    rounded[j][:, c0 - s0 : c1 - s0, :].rearrange("p (c i) r -> p c r i", i=RUN),
+                    rounded(j, c0, c1).rearrange("p (c i) r -> p c r i", i=RUN),
                     picked[j][:, :, c0 - s0 : c1 - s0].rearrange("p r (c i) -> p c r i", i=RUN),
                     factor.broadcast_to([P, (c1 - c0) // RUN, PACK, RUN]),
                     MULT,
                 )
 
         def quantize(j, c0, c1):
-            a, s0 = CHUNKS[j][:2]
+            a = CHUNKS[j][0]
             nc.vector.quantize_mx(
                 out=x_codes[a][:, c0:c1].bitcast(FP8X4),
                 scales=x_plane[:, a, c0:c1],
-                in_=rounded[j][:, c0 - s0 : c1 - s0, :].rearrange("p n r -> p (n r)"),
+                in_=rounded(j, c0, c1).rearrange("p n r -> p (n r)"),
             )
 
         def multiply(a, banks):
@@ -198,7 +212,9 @@ def tile_moe_pre_lin_none_kernel(tc, xT, w_words, w_scales, gate, offs, pos1, po
             gather_on_vector(j + 1, range(ahead))
             weigh(j)
             gather_on_vector(j + 1, range(ahead, PACK))
-            quantize(j, s0, s1)
+            calls = LATE_CALLS if j == last - 2 else CALLS
+            for c0, c1 in zip(calls, calls[1:]):
+                quantize(j, *((s1 - c1, s1 - c0) if s0 else (c0, c1)))
             multiply(a, [b for b in EARLY_BANKS if s0 <= BANKS[b][0] * C < s1])
         for a in range(PASSES - 1):
             multiply(a, LATE_BANKS)

@@ -31,9 +31,9 @@ WIDE = 1024
 TAIL = 2 * C
 
 THIRD_ROW = 352
-POOL_FULL = 576
-POOL_LATE, POOL_LAST = 448, 224
-LATE_ROW = 640
+POOL_FULL = 592
+POOL_LATE, POOL_LAST, POOL_TAIL = 472, 240, 64
+LATE_ROW = 704
 
 STEADY = [0, 0, THIRD_ROW, WIDE]
 CHUNKS = [
@@ -43,7 +43,7 @@ CHUNKS = [
     (1, WIDE, S, STEADY, POOL_FULL),
     (2, 0, WIDE, STEADY, POOL_LATE),
     (2, WIDE, S - TAIL, [0, 0, 0, LATE_ROW], POOL_LAST),
-    (2, S - TAIL, S, [0] * PACK, 0),
+    (2, S - TAIL, S, [0] * PACK, POOL_TAIL),
 ]
 CALLS = [0, 256, 640, WIDE]
 LATE_CALLS = [0, 512, WIDE]
@@ -69,7 +69,8 @@ def tile_moe_pre_lin_none_kernel(tc, xT, w_words, w_scales, gate, offs, pos1, po
         first_slots = keep.tile([P, T // GROUP], U16, name="first_slots")
         second_slots = keep.tile([P, T // GROUP], U16, name="second_slots")
         x_rows = [[keep.tile([P, T + PAD], F32, name="x_row_%d_%d" % (a, r)) for r in range(PACK)] for a in range(PASSES)]
-        pool_gates = {g0: keep.tile([P, POOL_FULL], F32, name="pool_gates_%d" % g0) for g0 in (WIDE - POOL_FULL, WIDE)}
+        gate_widths = {WIDE - POOL_FULL: POOL_FULL, WIDE: POOL_FULL, S - TAIL: POOL_TAIL}
+        pool_gates = {g0: keep.tile([P, n], F32, name="pool_gates_%d" % g0) for g0, n in gate_widths.items()}
         gate_rows = stage.tile([P, C], F32, name="gate_rows", tag="picked_1")
         gate_cols = keep.tile([P, E], F32, name="gate_cols")
         identity = keep.tile([P, P], F32, name="identity")
@@ -78,8 +79,7 @@ def tile_moe_pre_lin_none_kernel(tc, xT, w_words, w_scales, gate, offs, pos1, po
         x_codes = [keep.tile([P, S], U32, name="x_codes_%d" % a, align_bytes=64) for a in range(PASSES)]
         x_plane = keep.tile([P, PASSES, S], U8, name="x_plane", align_bytes=64)
         y = keep.tile([P, S], F32, name="y", align_bytes=64)
-        rounded_shared = keep.tile([P, WIDE, PACK], BF16, name="rounded_shared", align_bytes=64)
-        rounded_tail = keep.tile([P, TAIL, PACK], BF16, name="rounded_tail", align_bytes=64)
+        rounded_values = keep.tile([P, WIDE, PACK], BF16, name="rounded_values", align_bytes=64)
 
         idle = keep.tile([P, 2], F32, name="idle")
         nc.vector.memset(idle[:, 0:1], 0.0)
@@ -98,10 +98,14 @@ def tile_moe_pre_lin_none_kernel(tc, xT, w_words, w_scales, gate, offs, pos1, po
         nc.sync.dma_start(slot_tokens[:], offs)
         load_rows(0, range(1, PACK))
         nc.sync.dma_start(out=gate_rows[:], in_=gate[: P // E, :].rearrange("q (e c) -> (q e) c", c=C))
-        for g0 in pool_gates:
-            nc.sync.dma_start(out=pool_gates[g0][:], in_=gate[:P, g0 : g0 + POOL_FULL])
+        def load_gates(starts):
+            for g0 in starts:
+                nc.sync.dma_start(out=pool_gates[g0][:], in_=gate[:P, g0 : g0 + gate_widths[g0]])
+
+        load_gates([WIDE - POOL_FULL, WIDE])
         load_rows(1, range(PACK))
         load_rows(2, range(PACK))
+        load_gates([S - TAIL])
         scale_rows = w_scales.rearrange("e a q n -> a q e n")
         for quad in range(4):
             for a in range(PASSES):
@@ -147,14 +151,14 @@ def tile_moe_pre_lin_none_kernel(tc, xT, w_words, w_scales, gate, offs, pos1, po
                     nc.vector.tensor_copy(picked[j][:, r, cut - s0 :], x_rows[a][r][:].indirect(slot_tokens[:, cut // GROUP : s1 // GROUP]))
 
         def rounded(j, c0, c1):
-            s0, pool = CHUNKS[j][1], CHUNKS[j][4]
-            return (rounded_shared if pool else rounded_tail)[:, c0 - s0 : c1 - s0, :]
+            base = CHUNKS[j][1] - (TAIL if j == len(CHUNKS) - 1 else 0)
+            return rounded_values[:, c0 - base : c1 - base, :]
 
         def weigh(j):
             s0 = CHUNKS[j][1]
             (v0, v1), (p0, p1) = shares(j)
             if p1 > p0:
-                g0 = WIDE if s0 else WIDE - POOL_FULL
+                g0 = max(g for g in pool_gates if g <= p0)
                 nc.gpsimd.tensor_tensor(
                     rounded(j, p0, p1).rearrange("p (c i) r -> p c r i", i=RUN),
                     picked[j][:, :, p0 - s0 : p1 - s0].rearrange("p r (c i) -> p c r i", i=RUN),
@@ -221,7 +225,8 @@ def tile_moe_pre_lin_none_kernel(tc, xT, w_words, w_scales, gate, offs, pos1, po
 
         gather_on_scalar(last)
         weigh(last - 1)
-        quantize(last - 1, WIDE, WIDE + BANK)
+        quantize(last - 1, WIDE + TAIL, WIDE + BANK)
+        quantize(last - 1, WIDE, WIDE + TAIL)
         multiply(PASSES - 1, [2])
         weigh(last)
         quantize(last - 1, WIDE + BANK, S - TAIL)

@@ -25,6 +25,7 @@ PACK = 4
 PASSES = K // (P * PACK)
 GROUP = 16
 PAD = 16
+SKEW = 16
 RUN = 4
 BANK = 512
 WIDE = 1024
@@ -32,17 +33,18 @@ TAIL = 2 * C
 
 THIRD_ROW = 352
 POOL_FULL = 592
-POOL_LATE, POOL_LAST, POOL_TAIL = 472, 240, 64
-LATE_ROW = 704
+POOL_FIRST, FIRST_CUT = 624, 384
+FIRST_ORDER = [3, 2, 1, 0]
+POOL_LATE, POOL_LAST, POOL_TAIL = 480, 240, 64
 
 STEADY = [0, 0, THIRD_ROW, WIDE]
 CHUNKS = [
-    (0, 0, WIDE, [WIDE // 2] * PACK, POOL_FULL),
+    (0, 0, WIDE, None, POOL_FIRST),
     (0, WIDE, S, STEADY, POOL_FULL),
     (1, 0, WIDE, STEADY, POOL_FULL),
     (1, WIDE, S, STEADY, POOL_FULL),
     (2, 0, WIDE, STEADY, POOL_LATE),
-    (2, WIDE, S - TAIL, [0, 0, 0, LATE_ROW], POOL_LAST),
+    (2, WIDE, S - TAIL, [0, 0, 0, S - TAIL - WIDE], POOL_LAST),
     (2, S - TAIL, S, [0] * PACK, POOL_TAIL),
 ]
 CALLS = [0, 256, 640, WIDE]
@@ -69,7 +71,7 @@ def tile_moe_pre_lin_none_kernel(tc, xT, w_words, w_scales, gate, offs, pos1, po
         first_slots = keep.tile([P, T // GROUP], U16, name="first_slots")
         second_slots = keep.tile([P, T // GROUP], U16, name="second_slots")
         x_rows = [[keep.tile([P, T + PAD], F32, name="x_row_%d_%d" % (a, r)) for r in range(PACK)] for a in range(PASSES)]
-        gate_widths = {WIDE - POOL_FULL: POOL_FULL, WIDE: POOL_FULL, S - TAIL: POOL_TAIL}
+        gate_widths = {WIDE - POOL_FIRST: POOL_FIRST, WIDE: POOL_FULL, S - TAIL: POOL_TAIL}
         pool_gates = {g0: keep.tile([P, n], F32, name="pool_gates_%d" % g0) for g0, n in gate_widths.items()}
         gate_rows = stage.tile([P, C], F32, name="gate_rows", tag="picked_1")
         gate_cols = keep.tile([P, E], F32, name="gate_cols")
@@ -94,15 +96,15 @@ def tile_moe_pre_lin_none_kernel(tc, xT, w_words, w_scales, gate, offs, pos1, po
             for r in rows:
                 nc.sync.dma_start(out=x_rows[a][r][:, :T], in_=x_view[a, r])
 
-        load_rows(0, [0])
+        load_rows(0, FIRST_ORDER[:1])
         nc.sync.dma_start(slot_tokens[:], offs)
-        load_rows(0, range(1, PACK))
+        load_rows(0, FIRST_ORDER[1:])
         nc.sync.dma_start(out=gate_rows[:], in_=gate[: P // E, :].rearrange("q (e c) -> (q e) c", c=C))
         def load_gates(starts):
             for g0 in starts:
                 nc.sync.dma_start(out=pool_gates[g0][:], in_=gate[:P, g0 : g0 + gate_widths[g0]])
 
-        load_gates([WIDE - POOL_FULL, WIDE])
+        load_gates([WIDE - POOL_FIRST, WIDE])
         load_rows(1, range(PACK))
         load_rows(2, range(PACK))
         load_gates([S - TAIL])
@@ -135,20 +137,30 @@ def tile_moe_pre_lin_none_kernel(tc, xT, w_words, w_scales, gate, offs, pos1, po
         sums = {}
         issued = [0] * len(BANKS)
 
+        def stage_chunk(j):
+            s0, s1 = CHUNKS[j][1:3]
+            picked[j] = stage.tile([P, PACK, s1 - s0 + SKEW], F32, name="picked", tag="picked_%d" % (j % 2))
+
+        def gather(on_scalar, j, r, c0, c1):
+            a, s0 = CHUNKS[j][:2]
+            window = x_rows[a][r][:].indirect(slot_tokens[:, c0 // GROUP : c1 // GROUP])
+            if on_scalar:
+                nc.scalar.activation(picked[j][:, r, c0 - s0 : c1 - s0], window, COPY)
+            else:
+                nc.vector.tensor_copy(picked[j][:, r, c0 - s0 : c1 - s0], window)
+
         def gather_on_scalar(j):
             a, s0, s1, own, pool = CHUNKS[j]
-            picked[j] = stage.tile([P, PACK, s1 - s0], F32, name="picked", tag="picked_%d" % (j % 2))
+            stage_chunk(j)
             for r in range(PACK):
-                cut = s1 - own[r]
-                if cut > s0:
-                    nc.scalar.activation(picked[j][:, r, : cut - s0], x_rows[a][r][:].indirect(slot_tokens[:, s0 // GROUP : cut // GROUP]), COPY)
+                if s1 - own[r] > s0:
+                    gather(True, j, r, s0, s1 - own[r])
 
         def gather_on_vector(j, rows):
             a, s0, s1, own, pool = CHUNKS[j]
             for r in rows:
-                cut = s1 - own[r]
-                if cut < s1:
-                    nc.vector.tensor_copy(picked[j][:, r, cut - s0 :], x_rows[a][r][:].indirect(slot_tokens[:, cut // GROUP : s1 // GROUP]))
+                if own[r]:
+                    gather(False, j, r, s1 - own[r], s1)
 
         def rounded(j, c0, c1):
             base = CHUNKS[j][1] - (TAIL if j == len(CHUNKS) - 1 else 0)
@@ -165,7 +177,7 @@ def tile_moe_pre_lin_none_kernel(tc, xT, w_words, w_scales, gate, offs, pos1, po
                     pool_gates[g0][:, p0 - g0 : p1 - g0].rearrange("p (c o i) -> p c o i", o=1, i=RUN).broadcast_to([P, (p1 - p0) // RUN, PACK, RUN]),
                     MULT,
                 )
-            cuts = [v0] + [c for c in range(BANK, v1, BANK) if c > v0] + [v1]
+            cuts = [v0] + [c for c in range(BANK, v1, BANK) if c > v0] + [v1] if j else [v0, CALLS[1], v1]
             for c0, c1 in zip(cuts, cuts[1:]):
                 b = c0 // BANK
                 factor = gate_banks[b][:, c0 - b * BANK : c1 - b * BANK].rearrange("p (c o i) -> p c o i", o=1, i=RUN)
@@ -207,8 +219,10 @@ def tile_moe_pre_lin_none_kernel(tc, xT, w_words, w_scales, gate, offs, pos1, po
             engine_copy(out=y[:, e0 * C : e1 * C], in_=sums[b][:])
 
         last = len(CHUNKS) - 1
-        gather_on_scalar(0)
-        gather_on_vector(0, range(PACK))
+        stage_chunk(0)
+        for r, c0, c1 in [(r, 0, WIDE) for r in FIRST_ORDER[:-1]] + [(0, FIRST_CUT, WIDE), (0, 0, FIRST_CUT)]:
+            gather(True, 0, r, c0, (c0 + c1) // 2)
+            gather(False, 0, r, (c0 + c1) // 2, c1)
         for j in range(last - 1):
             a, s0, s1 = CHUNKS[j][:3]
             gather_on_scalar(j + 1)

@@ -31,19 +31,19 @@ BANK = 512
 WIDE = 1024
 TAIL = 2 * C
 
-THIRD_ROW = 352
-POOL_FULL = 592
-POOL_FIRST, FIRST_CUT = 624, 384
+THIRD_ROW = (384, 352)
+POOL_FULL = 600
+POOL_FIRST, FIRST_CUT = 608, 384
 FIRST_ORDER = [3, 2, 1, 0]
 POOL_LATE, POOL_LAST, POOL_TAIL = 480, 240, 64
 
-STEADY = [0, 0, THIRD_ROW, WIDE]
+STEADY = [[0, 0, n, WIDE] for n in THIRD_ROW]
 CHUNKS = [
     (0, 0, WIDE, None, POOL_FIRST),
-    (0, WIDE, S, STEADY, POOL_FULL),
-    (1, 0, WIDE, STEADY, POOL_FULL),
-    (1, WIDE, S, STEADY, POOL_FULL),
-    (2, 0, WIDE, STEADY, POOL_LATE),
+    (0, WIDE, S, STEADY[0], POOL_FULL),
+    (1, 0, WIDE, STEADY[1], POOL_FULL),
+    (1, WIDE, S, STEADY[0], POOL_FULL),
+    (2, 0, WIDE, STEADY[1], POOL_LATE),
     (2, WIDE, S - TAIL, [0, 0, 0, S - TAIL - WIDE], POOL_LAST),
     (2, S - TAIL, S, [0] * PACK, POOL_TAIL),
 ]

@@ -31,9 +31,9 @@ BANK = 512
 WIDE = 1024
 TAIL = 2 * C
 
-THIRD_ROW = (384, 352)
+THIRD_ROW = (448, 384, 384, 352)
 POOL_FULL = 600
-POOL_FIRST, FIRST_CUT = 608, 384
+POOL_FIRST, FIRST_CUT = 624, 384
 FIRST_ORDER = [3, 2, 1, 0]
 POOL_LATE, POOL_LAST, POOL_TAIL = 480, 240, 64
 
@@ -42,8 +42,8 @@ CHUNKS = [
     (0, 0, WIDE, None, POOL_FIRST),
     (0, WIDE, S, STEADY[0], POOL_FULL),
     (1, 0, WIDE, STEADY[1], POOL_FULL),
-    (1, WIDE, S, STEADY[0], POOL_FULL),
-    (2, 0, WIDE, STEADY[1], POOL_LATE),
+    (1, WIDE, S, STEADY[2], POOL_FULL),
+    (2, 0, WIDE, STEADY[3], POOL_LATE),
     (2, WIDE, S - TAIL, [0, 0, 0, S - TAIL - WIDE], POOL_LAST),
     (2, S - TAIL, S, [0] * PACK, POOL_TAIL),
 ]

from contextlib import ExitStack

import concourse.mybir as mybir
from concourse.masks import make_identity

K, T, E, C, N = 1536, 1024, 16, 128, 128
S = E * C

FLOPS = 2 * K * S * N
BYTES = 4 * K * T + E * K * N + E * (K // 32) * N + 4 * S + 2 * 128 * (S + 2 * T) // 16 + 4 * N * T

F32 = mybir.dt.float32
BF16 = mybir.dt.bfloat16
I32 = mybir.dt.int32
U32 = mybir.dt.uint32
U16 = mybir.dt.uint16
U8 = mybir.dt.uint8
FP8X4 = mybir.dt.float8_e4m3fn_x4
MULT = mybir.AluOpType.mult
ADD = mybir.AluOpType.add
COPY = mybir.ActivationFunctionType.Copy

P = 128
PACK = 4
PASSES = K // (P * PACK)
GROUP = 16
PAD = 16
SKEW = 16
RUN = 4
BANK = 512
WIDE = 1024
TAIL = 2 * C

THIRD_ROW = (448, 384, 384, 352)
POOL_FULL = 600
POOL_FIRST, FIRST_CUT = 624, 384
FIRST_ORDER = [3, 2, 1, 0]
POOL_LATE, POOL_LAST, POOL_TAIL = 480, 240, 64

STEADY = [[0, 0, n, WIDE] for n in THIRD_ROW]
CHUNKS = [
    (0, 0, WIDE, None, POOL_FIRST),
    (0, WIDE, S, STEADY[0], POOL_FULL),
    (1, 0, WIDE, STEADY[1], POOL_FULL),
    (1, WIDE, S, STEADY[2], POOL_FULL),
    (2, 0, WIDE, STEADY[3], POOL_LATE),
    (2, WIDE, S - TAIL, [0, 0, 0, S - TAIL - WIDE], POOL_LAST),
    (2, S - TAIL, S, [0] * PACK, POOL_TAIL),
]
CALLS = [0, 256, 640, WIDE]
LATE_CALLS = [0, 512, WIDE]
BANKS = [(0, 4), (4, 8), (8, 12), (12, 14), (14, 15), (15, 16)]
BANK_TAGS = ["sums_0", "sums_1", "sums_2", "sums_3", "gates_0", "gates_1"]
EARLY_BANKS, LATE_BANKS = range(4), (4, 5)
BACK = [0, 192, 576, 896, T]


def shares(j):
    a, s0, s1, own, pool = CHUNKS[j]
    return ((s0 + pool, s1), (s0, s0 + pool)) if s0 else ((s0, s1 - pool), (s1 - pool, s1))


def tile_moe_pre_lin_none_kernel(tc, xT, w_words, w_scales, gate, offs, pos1, pos2, out):
    nc = tc.nc
    with ExitStack() as ctx:
        keep = ctx.enter_context(tc.tile_pool(name="keep", bufs=1))
        stage = ctx.enter_context(tc.tile_pool(name="stage", bufs=1))
        psum = ctx.enter_context(tc.psum_pool(name="psum", bufs=1))

        slot_tokens = keep.tile([P, S // GROUP], U16, name="slot_tokens")
        first_slots = keep.tile([P, T // GROUP], U16, name="first_slots")
        second_slots = keep.tile([P, T // GROUP], U16, name="second_slots")
        x_rows = [[keep.tile([P, T + PAD], F32, name="x_row_%d_%d" % (a, r)) for r in range(PACK)] for a in range(PASSES)]
        gate_widths = {WIDE - POOL_FIRST: POOL_FIRST, WIDE: POOL_FULL, S - TAIL: POOL_TAIL}
        pool_gates = {g0: keep.tile([P, n], F32, name="pool_gates_%d" % g0) for g0, n in gate_widths.items()}
        gate_rows = stage.tile([P, C], F32, name="gate_rows", tag="picked_1")
        gate_cols = keep.tile([P, E], F32, name="gate_cols")
        identity = keep.tile([P, P], F32, name="identity")
        w_codes = keep.tile([P, E * PASSES, N], U32, name="w_codes", align_bytes=64)
        w_plane = keep.tile([P, E, N], U8, name="w_plane", align_bytes=64)
        x_codes = [keep.tile([P, S], U32, name="x_codes_%d" % a, align_bytes=64) for a in range(PASSES)]
        x_plane = keep.tile([P, PASSES, S], U8, name="x_plane", align_bytes=64)
        y = keep.tile([P, S], F32, name="y", align_bytes=64)
        rounded_values = keep.tile([P, WIDE, PACK], BF16, name="rounded_values", align_bytes=64)

        idle = keep.tile([P, 2], F32, name="idle")
        nc.vector.memset(idle[:, 0:1], 0.0)
        nc.scalar.activation(idle[:, 1:2], idle[:, 0:1], COPY)

        nc.vector.memset(w_plane[:].bitcast(I32), 0)
        make_identity(nc, identity[:])

        x_view = xT.rearrange("(a p r) t -> a r p t", p=P, r=PACK)

        def load_rows(a, rows):
            for r in rows:
                nc.sync.dma_start(out=x_rows[a][r][:, :T], in_=x_view[a, r])

        load_rows(0, FIRST_ORDER[:1])
        nc.sync.dma_start(slot_tokens[:], offs)
        load_rows(0, FIRST_ORDER[1:])
        nc.sync.dma_start(out=gate_rows[:], in_=gate[: P // E, :].rearrange("q (e c) -> (q e) c", c=C))
        def load_gates(starts):
            for g0 in starts:
                nc.sync.dma_start(out=pool_gates[g0][:], in_=gate[:P, g0 : g0 + gate_widths[g0]])

        load_gates([WIDE - POOL_FIRST, WIDE])
        load_rows(1, range(PACK))
        load_rows(2, range(PACK))
        load_gates([S - TAIL])
        scale_rows = w_scales.rearrange("e a q n -> a q e n")
        for quad in range(4):
            for a in range(PASSES):
                nc.sync.dma_start(out=w_plane[32 * quad + 4 * a : 32 * quad + 4 * a + 4].bitcast(I32),
                                  in_=scale_rows[a, 4 * quad : 4 * quad + 4].bitcast(I32))
        word_rows = w_words.rearrange("e a p n r -> p (e a) (n r)").bitcast(I32)
        for e0 in range(0, E, 4):
            rows = slice(e0 * PASSES, (e0 + 4) * PASSES)
            nc.sync.dma_start(out=w_codes[:, rows, :].bitcast(I32), in_=word_rows[:, rows, :])
        nc.sync.dma_start(first_slots[:], pos1)
        nc.sync.dma_start(second_slots[:], pos2)

        turned = psum.tile([P, C], F32, name="turned", tag="sums_0")
        nc.tensor.transpose(turned[:], gate_rows[:], identity[:])
        nc.vector.tensor_copy(gate_cols[:], turned[:, :E])
        gate_banks = [psum.tile([P, BANK], F32, name="gate_bank", tag="gates_%d" % b) for b in range(S // BANK)]
        spread = []
        for j in range(len(CHUNKS)):
            v0, v1 = shares(j)[0]
            for e in range(v0 // C, -(-v1 // C)):
                if e not in spread:
                    spread.append(e)
                    b, m = divmod(e, BANK // C)
                    nc.tensor.transpose(gate_banks[b][:, m * C : (m + 1) * C], gate_cols[:, e : e + 1].to_broadcast([P, P]), identity[:])

        picked = {}
        sums = {}
        issued = [0] * len(BANKS)

        def stage_chunk(j):
            s0, s1 = CHUNKS[j][1:3]
            picked[j] = stage.tile([P, PACK, s1 - s0 + SKEW], F32, name="picked", tag="picked_%d" % (j % 2))

        def gather(on_scalar, j, r, c0, c1):
            a, s0 = CHUNKS[j][:2]
            window = x_rows[a][r][:].indirect(slot_tokens[:, c0 // GROUP : c1 // GROUP])
            if on_scalar:
                nc.scalar.activation(picked[j][:, r, c0 - s0 : c1 - s0], window, COPY)
            else:
                nc.vector.tensor_copy(picked[j][:, r, c0 - s0 : c1 - s0], window)

        def gather_on_scalar(j):
            a, s0, s1, own, pool = CHUNKS[j]
            stage_chunk(j)
            for r in range(PACK):
                if s1 - own[r] > s0:
                    gather(True, j, r, s0, s1 - own[r])

        def gather_on_vector(j, rows):
            a, s0, s1, own, pool = CHUNKS[j]
            for r in rows:
                if own[r]:
                    gather(False, j, r, s1 - own[r], s1)

        def rounded(j, c0, c1):
            base = CHUNKS[j][1] - (TAIL if j == len(CHUNKS) - 1 else 0)
            return rounded_values[:, c0 - base : c1 - base, :]

        def weigh(j):
            s0 = CHUNKS[j][1]
            (v0, v1), (p0, p1) = shares(j)
            if p1 > p0:
                g0 = max(g for g in pool_gates if g <= p0)
                nc.gpsimd.tensor_tensor(
                    rounded(j, p0, p1).rearrange("p (c i) r -> p c r i", i=RUN),
                    picked[j][:, :, p0 - s0 : p1 - s0].rearrange("p r (c i) -> p c r i", i=RUN),
                    pool_gates[g0][:, p0 - g0 : p1 - g0].rearrange("p (c o i) -> p c o i", o=1, i=RUN).broadcast_to([P, (p1 - p0) // RUN, PACK, RUN]),
                    MULT,
                )
            cuts = [v0] + [c for c in range(BANK, v1, BANK) if c > v0] + [v1] if j else [v0, CALLS[1], v1]
            for c0, c1 in zip(cuts, cuts[1:]):
                b = c0 // BANK
                factor = gate_banks[b][:, c0 - b * BANK : c1 - b * BANK].rearrange("p (c o i) -> p c o i", o=1, i=RUN)
                nc.vector.tensor_tensor(
                    rounded(j, c0, c1).rearrange("p (c i) r -> p c r i", i=RUN),
                    picked[j][:, :, c0 - s0 : c1 - s0].rearrange("p r (c i) -> p c r i", i=RUN),
                    factor.broadcast_to([P, (c1 - c0) // RUN, PACK, RUN]),
                    MULT,
                )

        def quantize(j, c0, c1):
            a = CHUNKS[j][0]
            nc.vector.quantize_mx(
                out=x_codes[a][:, c0:c1].bitcast(FP8X4),
                scales=x_plane[:, a, c0:c1],
                in_=rounded(j, c0, c1).rearrange("p n r -> p (n r)"),
            )

        def multiply(a, banks):
            for b in banks:
                e0, e1 = BANKS[b]
                if b not in sums:
                    sums[b] = psum.tile([P, (e1 - e0) * C], F32, name="sums", tag=BANK_TAGS[b])
                for e in range(e0, e1):
                    cols = slice(e * C, (e + 1) * C)
                    nc.tensor.matmul_mx(
                        out=sums[b][:, (e - e0) * C : (e - e0 + 1) * C],
                        lhsT=w_codes[:, e * PASSES + a, :].bitcast(FP8X4),
                        lhsT_scale=w_plane[4 * a :, e, :],
                        rhs=x_codes[a][:, cols].bitcast(FP8X4),
                        rhs_scale=x_plane[:, a, cols],
                        start=(issued[b] == 0),
                        stop=(issued[b] == PASSES * (e1 - e0) - 1),
                    )
                    issued[b] += 1

        def copy_out(engine_copy, b):
            e0, e1 = BANKS[b]
            engine_copy(out=y[:, e0 * C : e1 * C], in_=sums[b][:])

        last = len(CHUNKS) - 1
        stage_chunk(0)
        for r, c0, c1 in [(r, 0, WIDE) for r in FIRST_ORDER[:-1]] + [(0, FIRST_CUT, WIDE), (0, 0, FIRST_CUT)]:
            gather(True, 0, r, c0, (c0 + c1) // 2)
            gather(False, 0, r, (c0 + c1) // 2, c1)
        for j in range(last - 1):
            a, s0, s1 = CHUNKS[j][:3]
            gather_on_scalar(j + 1)
            ahead = PACK if j == 0 else PACK - 1
            gather_on_vector(j + 1, range(ahead))
            weigh(j)
            gather_on_vector(j + 1, range(ahead, PACK))
            calls = LATE_CALLS if j == last - 2 else CALLS
            for c0, c1 in zip(calls, calls[1:]):
                quantize(j, *((s1 - c1, s1 - c0) if s0 else (c0, c1)))
            multiply(a, [b for b in EARLY_BANKS if s0 <= BANKS[b][0] * C < s1])
        for a in range(PASSES - 1):
            multiply(a, LATE_BANKS)

        gather_on_scalar(last)
        weigh(last - 1)
        quantize(last - 1, WIDE + TAIL, WIDE + BANK)
        quantize(last - 1, WIDE, WIDE + TAIL)
        multiply(PASSES - 1, [2])
        weigh(last)
        quantize(last - 1, WIDE + BANK, S - TAIL)
        multiply(PASSES - 1, [3])
        quantize(last, S - TAIL, S)
        multiply(PASSES - 1, LATE_BANKS)
        for b in range(len(BANKS) - 1):
            copy_out(nc.scalar.copy, b)
        copy_out(nc.vector.tensor_copy, len(BANKS) - 1)

        first_results = stage.tile([P, T], F32, name="first_results", tag="picked_0")
        total = stage.tile([P, T], F32, name="total", tag="picked_1")
        pieces = list(zip(BACK, BACK[1:]))
        nc.vector.tensor_copy(first_results[:, : BACK[1]], y[:].indirect(first_slots[:, : BACK[1] // GROUP]))
        for t0, t1 in pieces[1:]:
            nc.scalar.activation(first_results[:, t0:t1], y[:].indirect(first_slots[:, t0 // GROUP : t1 // GROUP]), COPY)
        for t0, t1 in pieces:
            nc.vector.tensor_tensor(total[:, t0:t1], y[:].indirect(second_slots[:, t0 // GROUP : t1 // GROUP]), first_results[:, t0:t1], ADD)
        for t0, t1 in [(0, BACK[2])] + pieces[2:]:
            nc.sync.dma_start(out=out[:, t0:t1], in_=total[:, t0:t1])
